import numpy as np
import ml_dtypes


def mxq(x, axis, fmt="e4m3"):
    dtype, down = {"e4m3": (ml_dtypes.float8_e4m3fn, 7), "e5m2": (ml_dtypes.float8_e5m2, 14)}[fmt]
    v = np.moveaxis(np.asarray(x, np.float32).astype(ml_dtypes.bfloat16).astype(np.float64), axis, -1)
    blocks = v.reshape(v.shape[:-1] + (-1, 32))
    amax = np.abs(blocks).max(-1, keepdims=True)
    byte = np.maximum(np.where(amax > 0, np.frexp(amax)[1] - 1 + 127, 0) - down, 1)
    scale = np.exp2(byte - 127.0)
    codes = (blocks / scale).astype(np.float32).astype(dtype).astype(np.float64)
    return np.moveaxis((codes * scale).reshape(v.shape), -1, axis)


WIDE = False


def mx_kscale(k):
    if not WIDE:
        return np.ones(k)
    levels = np.array([10, -10, 5, -5, 0])
    if k % 512:
        return np.exp2(np.random.permutation(np.resize(levels, k // 32))).repeat(32)
    a = np.empty((k // 512, 16))
    for p in range(k // 512):
        a[p, :8] = np.random.permutation(np.resize(levels, 8))
        for g in range(8):
            far = levels[np.abs(levels - a[p, g]) >= 10]
            a[p, g + 8] = far[np.random.randint(len(far))]
    return np.exp2(a.ravel()).repeat(32)


def f64(x):
    return np.asarray(x).astype(np.float64)


def striped(idx):
    return np.tile(np.asarray(idx).reshape(-1, 16).T, (8, 1)).astype(np.uint16)


def unstriped(offs):
    return offs[:16].T.reshape(-1).astype(np.int64)


E2M1 = np.array([0.0, 0.5, 1.0, 1.5, 2.0, 3.0, 4.0, 6.0, -0.0, -0.5, -1.0, -1.5, -2.0, -3.0, -4.0, -6.0])


def pack_weight(w, fmt):
    k, n = w.shape
    w = f64(np.asarray(w, np.float32).astype(ml_dtypes.bfloat16)).reshape(k // 32, 32, n)
    amax = np.abs(w).max(1)
    if fmt == "e4m3":
        byte = np.frexp(amax)[1] - 1 + 127 - 7
    else:
        mant, ex = np.frexp(amax / 6.0)
        byte = np.where(mant > 0.5, ex, ex - 1) + 127
    byte = np.clip(np.where(amax > 0, byte, 1), 1, 254)
    scaled = (w * np.exp2(127.0 - byte)[:, None, :]).reshape(k, n).astype(np.float32)
    by_word = np.ascontiguousarray(scaled.reshape(k // 512, 128, 4, n).transpose(0, 1, 3, 2))
    if fmt == "e4m3":
        words = by_word.astype(ml_dtypes.float8_e4m3fn).view(np.uint8)
    else:
        c = by_word.astype(ml_dtypes.float4_e2m1fn).view(np.uint8) & 0xF
        words = (c[..., 0::2] | (c[..., 1::2] << 4)).reshape(k // 512, 128, 2 * n)
    return np.ascontiguousarray(words), np.ascontiguousarray(byte.astype(np.uint8).reshape(k // 512, 16, n))


def unpack_weight(words, scales, fmt):
    g, _, n = scales.shape
    words = np.ascontiguousarray(words).reshape(g, 128, n, -1)
    if fmt == "e4m3":
        vals = words.view(ml_dtypes.float8_e4m3fn).astype(np.float64)
    else:
        nib = np.empty((g, 128, n, 4), np.uint8)
        nib[..., 0::2] = words & 0xF
        nib[..., 1::2] = words >> 4
        vals = E2M1[nib]
    vals = vals * np.repeat(np.exp2(scales.astype(np.float64) - 127.0), 8, axis=1)[..., None]
    return vals.transpose(0, 1, 3, 2).reshape(g * 512, n)


def bf(x):
    return np.asarray(x, np.float32).astype(ml_dtypes.bfloat16)


def planes(Y):
    r, m = Y.shape
    b = f64(bf(Y)).reshape(r // 32, 32, m)
    amax = np.abs(b).max(1)
    byte = np.clip(np.where(amax > 0, np.frexp(amax)[1] - 1 + 127 - 7, 1), 1, 254)
    codes = (b * np.exp2(127.0 - byte)[:, None, :]).reshape(r, m).astype(np.float32).astype(ml_dtypes.float8_e4m3fn).view(np.uint8)
    words = codes.reshape(r // 512, 128, 4, m).transpose(0, 1, 3, 2)
    return np.ascontiguousarray(words), np.ascontiguousarray(byte.astype(np.uint8).reshape(r // 512, 16, m))


B, N, T, D, NQ = 1, 512, 2048, 512, 512


def setup_inputs():
    n = np.random.standard_normal
    jdx = np.random.permutation(1024)[:B * NQ]
    idx = np.random.permutation(T)[:B * N]
    s = mx_kscale(D)[:, None]
    kp = pack_weight(n((D, T)) / s, "e4m3")
    return {
        "qT": (n((D, 1024)) * s * (1.00 / np.sqrt(D))).astype(np.float32),
        "k_words": kp[0],
        "k_scales": kp[1],
        "ls": (np.random.uniform(7.8, 8.4, (B, 1, NQ))).astype(np.float32),
        "offq": striped(jdx),
        "offs": striped(idx),
    }


def reference(qT, k_words, k_scales, ls, offq, offs):
    jdx = unstriped(offq)
    idx = unstriped(offs)
    pick = lambda x, which: x[:, which].reshape(x.shape[0], B, -1).transpose(1, 0, 2)
    qg = mxq(pick(f64(qT), jdx), 1, "e4m3")
    k = unpack_weight(k_words, k_scales, "e4m3")
    kg = pick(k, idx)
    qq = qg
    a = kg.transpose(0, 2, 1) @ qq
    y = np.exp(a - f64(ls))
    Y = y[0]
    words, scales = planes(Y)
    return Y, words, scales

@@ -1,0 +1,188 @@
+from contextlib import ExitStack
+
+import concourse.mybir as mybir
+from concourse.masks import make_identity
+
+F32 = mybir.dt.float32
+BF16 = mybir.dt.bfloat16
+I32 = mybir.dt.int32
+U32 = mybir.dt.uint32
+U16 = mybir.dt.uint16
+U8 = mybir.dt.uint8
+FP8X4 = mybir.dt.float8_e4m3fn_x4
+COPY = mybir.ActivationFunctionType.Copy
+EXP = mybir.ActivationFunctionType.Exp
+SUB = mybir.AluOpType.subtract
+
+P = 128
+PACK = 4
+D = 512
+POOL_Q = 1024
+POOL_K = 2048
+NQ = 512
+N = 512
+HALF = NQ // 2
+CHUNK = 128
+CAST_COLS = POOL_Q // 2
+LAST_ON_SCALAR = 160
+
+FLOPS = 2 * D * N * NQ
+
+
+def tile_attend_plw_lq_topk_kernel(tc, qT, k_words, k_scales, ls, offq, offs, out_0, out_1, out_2):
+    nc = tc.nc
+    with ExitStack() as ctx:
+        sb = ctx.enter_context(tc.tile_pool(name="sb", bufs=1))
+        ps = ctx.enter_context(tc.psum_pool(name="ps", bufs=1))
+
+        q_rows = qT.rearrange("(p t) c -> p t c", t=PACK)
+        raw = {}
+
+        def load_q(u, h):
+            raw[u, h] = sb.tile([P, 2, CAST_COLS], F32, name=f"raw{u}{h}")
+            nc.sync.dma_start(raw[u, h][:], q_rows[:, 2 * u : 2 * u + 2, h * CAST_COLS : (h + 1) * CAST_COLS])
+
+        scale_pool = sb.tile([P, POOL_K], U8, name="scale_pool")
+        nc.vector.memset(scale_pool[:].bitcast(I32), 0)
+        ls_cols = sb.tile([P, PACK], F32, name="ls_cols")
+        nc.scalar.dma_start(ls_cols[:], ls.rearrange("a b (p c) -> p (a b c)", c=PACK))
+        k_list = sb.tile([P, N // 16], U16, name="k_list")
+        nc.sync.dma_start(k_list[:], offs)
+        load_q(0, 0)
+        for g in range(4):
+            nc.sync.dma_start(
+                scale_pool[32 * g : 32 * g + 4, :].bitcast(I32),
+                k_scales[0, 4 * g : 4 * g + 4, :].bitcast(I32),
+            )
+        load_q(0, 1)
+        q_list = sb.tile([P, NQ // 16], U16, name="q_list")
+        nc.sync.dma_start(q_list[:], offq)
+        load_q(1, 0)
+        load_q(1, 1)
+        key_pool = sb.tile([P, POOL_K], I32, name="key_pool")
+        nc.sync.dma_start(key_pool[:], k_words[0].rearrange("p n t -> p (n t)").bitcast(I32))
+
+        ident = sb.tile([P, P], F32, name="ident")
+        make_identity(nc, ident[:])
+
+        pairs = [sb.tile([P, POOL_Q, 2], BF16, name=f"pairs{u}") for u in range(2)]
+
+        def cast_scalar(u, h, a, b):
+            nc.scalar.activation(
+                pairs[u][:, h * CAST_COLS + a : h * CAST_COLS + b, :],
+                raw[u, h][:, :, a:b].rearrange("p t c -> p c t"),
+                COPY,
+            )
+
+        cast_scalar(0, 0, 0, CAST_COLS)
+        cast_scalar(0, 1, 0, CAST_COLS)
+        cast_scalar(1, 0, 0, CAST_COLS)
+
+        ls_bank = ps.tile([P, PACK, P], F32, name="ls_bank")
+        for c in range(PACK):
+            nc.tensor.transpose(ls_bank[:, c, :], ls_cols[:, c : c + 1].to_broadcast([P, P]), ident[:])
+        ls_rows = sb.tile([P, NQ], F32, name="ls_rows")
+        nc.vector.tensor_copy(ls_rows[:].rearrange("p (n c) -> p n c", c=PACK), ls_bank[:].rearrange("p c n -> p n c"))
+
+        ks_listed = sb.tile([P, N], U8, name="ks_listed")
+        nc.vector.tensor_copy(ks_listed[:], scale_pool[:].indirect(k_list[:]))
+        ks_dealt = sb.tile([P, N], U8, name="ks_dealt", align_bytes=64)
+        nc.vector.tensor_copy(
+            ks_dealt[:].rearrange("p (r s) -> p s r", r=PACK),
+            ks_listed[:].rearrange("p (s r) -> p s r", r=PACK),
+        )
+
+        listed = [sb.tile([P, 2, HALF], U32, name=f"listed{h}") for h in range(2)]
+
+        def gather_q(u, h):
+            window = pairs[u][:].rearrange("p c t -> p (c t)").bitcast(U32)
+            nc.vector.tensor_copy(listed[h][:, u, :], window.indirect(q_list[:, h * (HALF // 16) : (h + 1) * (HALF // 16)]))
+
+        gather_q(0, 0)
+        gather_q(0, 1)
+
+        cast_scalar(1, 1, 0, LAST_ON_SCALAR)
+        nc.vector.tensor_copy(
+            pairs[1][:, CAST_COLS + LAST_ON_SCALAR :, :],
+            raw[1, 1][:, :, LAST_ON_SCALAR:].rearrange("p t c -> p c t"),
+        )
+        gather_q(1, 0)
+        gather_q(1, 1)
+
+        q_codes, q_scales = [], []
+        for h in range(2):
+            woven = sb.tile([P, HALF * PACK], BF16, name=f"woven{h}", align_bytes=64)
+            nc.scalar.copy(
+                woven[:].bitcast(U32).rearrange("p (c u) -> p c u", u=2),
+                listed[h][:].rearrange("p u c -> p c u"),
+            )
+            codes = sb.tile([P, HALF], U32, name=f"q_codes{h}", align_bytes=64)
+            scales = sb.tile([P, HALF], U8, name=f"q_scales{h}", align_bytes=64)
+            nc.vector.quantize_mx(codes[:].bitcast(FP8X4), scales[:], woven[:])
+            q_codes.append(codes)
+            q_scales.append(scales)
+
+        kw_dealt = sb.tile([P, N], U32, name="kw_dealt", align_bytes=64)
+        nc.vector.tensor_copy(
+            kw_dealt[:].rearrange("p (r s) -> p s r", r=PACK),
+            key_pool[:].bitcast(U32).indirect(k_list[:]),
+        )
+
+        y_codes = sb.tile([P, NQ], I32, name="y_codes", align_bytes=64)
+        y_scales = sb.tile([P, NQ], U8, name="y_scales", align_bytes=64)
+        y_rows = out_0.rearrange("(s r) q -> s r q", r=PACK)
+        words_out = out_1[0].rearrange("p q t -> p (q t)").bitcast(I32)
+        chunks = NQ // CHUNK
+        y = []
+
+        def scores(c):
+            bank = ps.tile([P, PACK, CHUNK], F32, name=f"bank{c}")
+            h, a = divmod(c * CHUNK, HALF)
+            for r in range(PACK):
+                nc.tensor.matmul_mx(
+                    bank[:, r, :],
+                    lhsT=kw_dealt[:, r * P : (r + 1) * P].bitcast(FP8X4),
+                    lhsT_scale=ks_dealt[:, r * P : (r + 1) * P],
+                    rhs=q_codes[h][:, a : a + CHUNK].bitcast(FP8X4),
+                    rhs_scale=q_scales[h][:, a : a + CHUNK],
+                    start=True,
+                    stop=True,
+                )
+            cols = slice(c * CHUNK, (c + 1) * CHUNK)
+            shifted = sb.tile([P, PACK, CHUNK], F32, name=f"shifted{c}")
+            nc.vector.tensor_tensor(shifted[:], bank[:], ls_rows[:, cols].unsqueeze(1).to_broadcast([P, PACK, CHUNK]), SUB)
+            y.append(sb.tile([P, PACK, CHUNK], F32, name=f"y{c}"))
+            nc.scalar.activation(y[c][:], shifted[:], EXP)
+            nc.sync.dma_start(y_rows[:, :, cols], y[c][:])
+
+        rounded = []
+
+        def weave(c):
+            rounded.append(sb.tile([P, CHUNK * PACK], BF16, name=f"rounded{c}", align_bytes=64))
+            nc.vector.tensor_copy(
+                rounded[c][:].rearrange("p (a i t) -> p a t i", i=4, t=PACK),
+                y[c][:].rearrange("p t (a i) -> p a t i", i=4),
+            )
+
+        def quantise(c):
+            cols = slice(c * CHUNK, (c + 1) * CHUNK)
+            nc.vector.quantize_mx(y_codes[:, cols].bitcast(FP8X4), y_scales[:, cols], rounded[c][:])
+
+        for c in range(chunks):
+            scores(c)
+        weave(0)
+        weave(1)
+        quantise(0)
+        quantise(1)
+        nc.sync.dma_start(words_out[:, :HALF], y_codes[:, :HALF])
+        weave(2)
+        weave(3)
+        quantise(2)
+        quantise(3)
+        nc.sync.dma_start(words_out[:, HALF:], y_codes[:, HALF:])
+        for g in range(4):
+            queue = nc.sync if g % 2 else nc.scalar
+            queue.dma_start(
+                out_2[0, 4 * g : 4 * g + 4, :].bitcast(I32),
+                y_scales[32 * g : 32 * g + 4, :].bitcast(I32),
+            )

@@ -24,7 +24,7 @@ N = 512
 HALF = NQ // 2
 CHUNK = 128
 CAST_COLS = POOL_Q // 2
-LAST_ON_SCALAR = 160
+LAST_ON_SCALAR = 256
 
 FLOPS = 2 * D * N * NQ
 
@@ -43,23 +43,23 @@ def tile_attend_plw_lq_topk_kernel(tc, qT, k_words, k_scales, ls, offq, offs, ou
             nc.sync.dma_start(raw[u, h][:], q_rows[:, 2 * u : 2 * u + 2, h * CAST_COLS : (h + 1) * CAST_COLS])
 
         scale_pool = sb.tile([P, POOL_K], U8, name="scale_pool")
-        nc.vector.memset(scale_pool[:].bitcast(I32), 0)
-        ls_cols = sb.tile([P, PACK], F32, name="ls_cols")
-        nc.scalar.dma_start(ls_cols[:], ls.rearrange("a b (p c) -> p (a b c)", c=PACK))
+        nc.gpsimd.memset(scale_pool[:].bitcast(I32), 0)
         k_list = sb.tile([P, N // 16], U16, name="k_list")
         nc.sync.dma_start(k_list[:], offs)
         load_q(0, 0)
+        q_list = sb.tile([P, NQ // 16], U16, name="q_list")
+        nc.sync.dma_start(q_list[:], offq)
         for g in range(4):
             nc.sync.dma_start(
                 scale_pool[32 * g : 32 * g + 4, :].bitcast(I32),
                 k_scales[0, 4 * g : 4 * g + 4, :].bitcast(I32),
             )
         load_q(0, 1)
-        q_list = sb.tile([P, NQ // 16], U16, name="q_list")
-        nc.sync.dma_start(q_list[:], offq)
         load_q(1, 0)
         load_q(1, 1)
-        key_pool = sb.tile([P, POOL_K], I32, name="key_pool")
+        ls_cols = sb.tile([P, PACK], F32, name="ls_cols")
+        nc.sync.dma_start(ls_cols[:], ls.rearrange("a b (p c) -> p (a b c)", c=PACK))
+        key_pool = sb.tile([P, POOL_K], I32, name="key_pool", tag="after_keys", align_bytes=64)
         nc.sync.dma_start(key_pool[:], k_words[0].rearrange("p n t -> p (n t)").bitcast(I32))
 
         ident = sb.tile([P, P], F32, name="ident")
@@ -81,8 +81,6 @@ def tile_attend_plw_lq_topk_kernel(tc, qT, k_words, k_scales, ls, offq, offs, ou
         ls_bank = ps.tile([P, PACK, P], F32, name="ls_bank")
         for c in range(PACK):
             nc.tensor.transpose(ls_bank[:, c, :], ls_cols[:, c : c + 1].to_broadcast([P, P]), ident[:])
-        ls_rows = sb.tile([P, NQ], F32, name="ls_rows")
-        nc.vector.tensor_copy(ls_rows[:].rearrange("p (n c) -> p n c", c=PACK), ls_bank[:].rearrange("p c n -> p n c"))
 
         ks_listed = sb.tile([P, N], U8, name="ks_listed")
         nc.vector.tensor_copy(ks_listed[:], scale_pool[:].indirect(k_list[:]))
@@ -92,41 +90,43 @@ def tile_attend_plw_lq_topk_kernel(tc, qT, k_words, k_scales, ls, offq, offs, ou
             ks_listed[:].rearrange("p (s r) -> p s r", r=PACK),
         )
 
-        listed = [sb.tile([P, 2, HALF], U32, name=f"listed{h}") for h in range(2)]
+        listed = sb.tile([P, 2, NQ], U32, name="listed", tag="after_weave", align_bytes=64)
 
-        def gather_q(u, h):
+        def gather_q(u, a, b):
             window = pairs[u][:].rearrange("p c t -> p (c t)").bitcast(U32)
-            nc.vector.tensor_copy(listed[h][:, u, :], window.indirect(q_list[:, h * (HALF // 16) : (h + 1) * (HALF // 16)]))
+            nc.vector.tensor_copy(listed[:, u, a:b], window.indirect(q_list[:, a // 16 : b // 16]))
 
-        gather_q(0, 0)
-        gather_q(0, 1)
-
+        gather_q(0, 0, NQ)
         cast_scalar(1, 1, 0, LAST_ON_SCALAR)
         nc.vector.tensor_copy(
             pairs[1][:, CAST_COLS + LAST_ON_SCALAR :, :],
             raw[1, 1][:, :, LAST_ON_SCALAR:].rearrange("p t c -> p c t"),
         )
-        gather_q(1, 0)
-        gather_q(1, 1)
+        gather_q(1, 0, HALF)
+        gather_q(1, HALF, NQ)
 
-        q_codes, q_scales = [], []
+        q_codes, q_scales, woven = [], [], []
         for h in range(2):
-            woven = sb.tile([P, HALF * PACK], BF16, name=f"woven{h}", align_bytes=64)
+            woven.append(sb.tile([P, HALF * PACK], BF16, name=f"woven{h}", align_bytes=64))
             nc.scalar.copy(
-                woven[:].bitcast(U32).rearrange("p (c u) -> p c u", u=2),
-                listed[h][:].rearrange("p u c -> p c u"),
+                woven[h][:].bitcast(U32).rearrange("p (c u) -> p c u", u=2),
+                listed[:, :, h * HALF : (h + 1) * HALF].rearrange("p u c -> p c u"),
             )
-            codes = sb.tile([P, HALF], U32, name=f"q_codes{h}", align_bytes=64)
-            scales = sb.tile([P, HALF], U8, name=f"q_scales{h}", align_bytes=64)
-            nc.vector.quantize_mx(codes[:].bitcast(FP8X4), scales[:], woven[:])
-            q_codes.append(codes)
-            q_scales.append(scales)
+        ls_rows = sb.tile([P, NQ], F32, name="ls_rows", tag="after_weave", align_bytes=64)
+        nc.scalar.copy(ls_rows[:].rearrange("p (n c) -> p n c", c=PACK), ls_bank[:].rearrange("p c n -> p n c"))
 
+        def quantise_q(h, tag):
+            q_codes.append(sb.tile([P, HALF], U32, name=f"q_codes{h}", tag=tag, align_bytes=64))
+            q_scales.append(sb.tile([P, HALF], U8, name=f"q_scales{h}", align_bytes=64))
+            nc.vector.quantize_mx(q_codes[h][:].bitcast(FP8X4), q_scales[h][:], woven[h][:])
+
+        quantise_q(0, "q_codes0")
         kw_dealt = sb.tile([P, N], U32, name="kw_dealt", align_bytes=64)
         nc.vector.tensor_copy(
             kw_dealt[:].rearrange("p (r s) -> p s r", r=PACK),
             key_pool[:].bitcast(U32).indirect(k_list[:]),
         )
+        quantise_q(1, "after_keys")
 
         y_codes = sb.tile([P, NQ], I32, name="y_codes", align_bytes=64)
         y_scales = sb.tile([P, NQ], U8, name="y_scales", align_bytes=64)
@@ -157,9 +157,9 @@ def tile_attend_plw_lq_topk_kernel(tc, qT, k_words, k_scales, ls, offq, offs, ou
 
         rounded = []
 
-        def weave(c):
-            rounded.append(sb.tile([P, CHUNK * PACK], BF16, name=f"rounded{c}", align_bytes=64))
-            nc.vector.tensor_copy(
+        def weave(c, copy, tag):
+            rounded.append(sb.tile([P, CHUNK * PACK], BF16, name=f"rounded{c}", tag=tag, align_bytes=64))
+            copy(
                 rounded[c][:].rearrange("p (a i t) -> p a t i", i=4, t=PACK),
                 y[c][:].rearrange("p t (a i) -> p a t i", i=4),
             )
@@ -170,16 +170,16 @@ def tile_attend_plw_lq_topk_kernel(tc, qT, k_words, k_scales, ls, offq, offs, ou
 
         for c in range(chunks):
             scores(c)
-        weave(0)
-        weave(1)
+        weave(0, nc.vector.tensor_copy, "after_weave")
+        weave(1, nc.vector.tensor_copy, "rounded1")
         quantise(0)
+        weave(2, nc.vector.tensor_copy, "rounded2")
         quantise(1)
-        nc.sync.dma_start(words_out[:, :HALF], y_codes[:, :HALF])
-        weave(2)
-        weave(3)
+        weave(3, nc.scalar.copy, "rounded3")
         quantise(2)
+        nc.sync.dma_start(words_out[:, : 3 * CHUNK], y_codes[:, : 3 * CHUNK])
         quantise(3)
-        nc.sync.dma_start(words_out[:, HALF:], y_codes[:, HALF:])
+        nc.sync.dma_start(words_out[:, 3 * CHUNK :], y_codes[:, 3 * CHUNK :])
         for g in range(4):
             queue = nc.sync if g % 2 else nc.scalar
             queue.dma_start(

@@ -24,7 +24,7 @@ N = 512
 HALF = NQ // 2
 CHUNK = 128
 CAST_COLS = POOL_Q // 2
-LAST_ON_SCALAR = 256
+ON_SCALAR = (320, 160)
 
 FLOPS = 2 * D * N * NQ
 
@@ -49,11 +49,7 @@ def tile_attend_plw_lq_topk_kernel(tc, qT, k_words, k_scales, ls, offq, offs, ou
         load_q(0, 0)
         q_list = sb.tile([P, NQ // 16], U16, name="q_list")
         nc.sync.dma_start(q_list[:], offq)
-        for g in range(4):
-            nc.sync.dma_start(
-                scale_pool[32 * g : 32 * g + 4, :].bitcast(I32),
-                k_scales[0, 4 * g : 4 * g + 4, :].bitcast(I32),
-            )
+        nc.sync.dma_start(scale_pool[0:P:8, :].bitcast(I32), k_scales[0].bitcast(I32))
         load_q(0, 1)
         load_q(1, 0)
         load_q(1, 1)
@@ -74,9 +70,15 @@ def tile_attend_plw_lq_topk_kernel(tc, qT, k_words, k_scales, ls, offq, offs, ou
                 COPY,
             )
 
+        def cast_shared(u):
+            split = ON_SCALAR[u]
+            cast_scalar(u, 1, 0, split)
+            nc.vector.tensor_copy(
+                pairs[u][:, CAST_COLS + split :, :],
+                raw[u, 1][:, :, split:].rearrange("p t c -> p c t"),
+            )
+
         cast_scalar(0, 0, 0, CAST_COLS)
-        cast_scalar(0, 1, 0, CAST_COLS)
-        cast_scalar(1, 0, 0, CAST_COLS)
 
         ls_bank = ps.tile([P, PACK, P], F32, name="ls_bank")
         for c in range(PACK):
@@ -90,99 +92,95 @@ def tile_attend_plw_lq_topk_kernel(tc, qT, k_words, k_scales, ls, offq, offs, ou
             ks_listed[:].rearrange("p (s r) -> p s r", r=PACK),
         )
 
+        for j in range(1, 4):
+            nc.sync.dma_start(ks_dealt[j:P:32, :].bitcast(I32), ks_dealt[8 * j : P : 32, :].bitcast(I32))
+
         listed = sb.tile([P, 2, NQ], U32, name="listed", tag="after_weave", align_bytes=64)
 
         def gather_q(u, a, b):
             window = pairs[u][:].rearrange("p c t -> p (c t)").bitcast(U32)
             nc.vector.tensor_copy(listed[:, u, a:b], window.indirect(q_list[:, a // 16 : b // 16]))
 
+        cast_shared(0)
         gather_q(0, 0, NQ)
-        cast_scalar(1, 1, 0, LAST_ON_SCALAR)
-        nc.vector.tensor_copy(
-            pairs[1][:, CAST_COLS + LAST_ON_SCALAR :, :],
-            raw[1, 1][:, :, LAST_ON_SCALAR:].rearrange("p t c -> p c t"),
-        )
-        gather_q(1, 0, HALF)
-        gather_q(1, HALF, NQ)
+        cast_scalar(1, 0, 0, CAST_COLS)
+        cast_shared(1)
+        gather_q(1, 0, CHUNK)
+        gather_q(1, CHUNK, NQ)
 
-        q_codes, q_scales, woven = [], [], []
-        for h in range(2):
-            woven.append(sb.tile([P, HALF * PACK], BF16, name=f"woven{h}", align_bytes=64))
+        woven = sb.tile([P, NQ * PACK], BF16, name="woven", align_bytes=64)
+        for a, b in ((0, CHUNK), (CHUNK, NQ)):
             nc.scalar.copy(
-                woven[h][:].bitcast(U32).rearrange("p (c u) -> p c u", u=2),
-                listed[:, :, h * HALF : (h + 1) * HALF].rearrange("p u c -> p c u"),
+                woven[:, a * PACK : b * PACK].bitcast(U32).rearrange("p (c u) -> p c u", u=2),
+                listed[:, :, a:b].rearrange("p u c -> p c u"),
             )
         ls_rows = sb.tile([P, NQ], F32, name="ls_rows", tag="after_weave", align_bytes=64)
         nc.scalar.copy(ls_rows[:].rearrange("p (n c) -> p n c", c=PACK), ls_bank[:].rearrange("p c n -> p n c"))
 
-        def quantise_q(h, tag):
-            q_codes.append(sb.tile([P, HALF], U32, name=f"q_codes{h}", tag=tag, align_bytes=64))
-            q_scales.append(sb.tile([P, HALF], U8, name=f"q_scales{h}", align_bytes=64))
-            nc.vector.quantize_mx(q_codes[h][:].bitcast(FP8X4), q_scales[h][:], woven[h][:])
-
-        quantise_q(0, "q_codes0")
+        q_scales = sb.tile([P, NQ], U8, name="q_scales", align_bytes=64)
+        first_codes = sb.tile([P, CHUNK], U32, name="first_codes", align_bytes=64)
+        nc.vector.quantize_mx(first_codes[:].bitcast(FP8X4), q_scales[:, :CHUNK], woven[:, : CHUNK * PACK])
         kw_dealt = sb.tile([P, N], U32, name="kw_dealt", align_bytes=64)
         nc.vector.tensor_copy(
             kw_dealt[:].rearrange("p (r s) -> p s r", r=PACK),
             key_pool[:].bitcast(U32).indirect(k_list[:]),
         )
-        quantise_q(1, "after_keys")
+        later_codes = sb.tile([P, NQ - CHUNK], U32, name="later_codes", tag="after_keys", align_bytes=64)
+        for a, b in ((CHUNK, HALF), (HALF, NQ)):
+            nc.vector.quantize_mx(
+                later_codes[:, a - CHUNK : b - CHUNK].bitcast(FP8X4), q_scales[:, a:b], woven[:, a * PACK : b * PACK]
+            )
 
         y_codes = sb.tile([P, NQ], I32, name="y_codes", align_bytes=64)
         y_scales = sb.tile([P, NQ], U8, name="y_scales", align_bytes=64)
         y_rows = out_0.rearrange("(s r) q -> s r q", r=PACK)
         words_out = out_1[0].rearrange("p q t -> p (q t)").bitcast(I32)
         chunks = NQ // CHUNK
-        y = []
+        last = chunks - 1
+        y = sb.tile([P, chunks, PACK, CHUNK], F32, name="y")
+        rounded = {}
+
+        def woven_order(tile):
+            return tile.rearrange("p (c a i t) -> p c a t i", a=CHUNK // 4, i=4, t=PACK)
+
+        def row_order(tile):
+            return tile.rearrange("p c t (a i) -> p c a t i", i=4)
 
         def scores(c):
             bank = ps.tile([P, PACK, CHUNK], F32, name=f"bank{c}")
-            h, a = divmod(c * CHUNK, HALF)
+            cols = slice(c * CHUNK, (c + 1) * CHUNK)
+            q_codes = later_codes[:, (c - 1) * CHUNK : c * CHUNK] if c else first_codes[:]
             for r in range(PACK):
                 nc.tensor.matmul_mx(
                     bank[:, r, :],
                     lhsT=kw_dealt[:, r * P : (r + 1) * P].bitcast(FP8X4),
                     lhsT_scale=ks_dealt[:, r * P : (r + 1) * P],
-                    rhs=q_codes[h][:, a : a + CHUNK].bitcast(FP8X4),
-                    rhs_scale=q_scales[h][:, a : a + CHUNK],
+                    rhs=q_codes.bitcast(FP8X4),
+                    rhs_scale=q_scales[:, cols],
                     start=True,
                     stop=True,
                 )
-            cols = slice(c * CHUNK, (c + 1) * CHUNK)
-            shifted = sb.tile([P, PACK, CHUNK], F32, name=f"shifted{c}")
-            nc.vector.tensor_tensor(shifted[:], bank[:], ls_rows[:, cols].unsqueeze(1).to_broadcast([P, PACK, CHUNK]), SUB)
-            y.append(sb.tile([P, PACK, CHUNK], F32, name=f"y{c}"))
-            nc.scalar.activation(y[c][:], shifted[:], EXP)
-            nc.sync.dma_start(y_rows[:, :, cols], y[c][:])
+            shifted = sb.tile([P, 1, PACK, CHUNK], F32, name=f"shifted{c}")
+            nc.vector.tensor_tensor(shifted[:, 0], bank[:], ls_rows[:, cols].unsqueeze(1).to_broadcast([P, PACK, CHUNK]), SUB)
+            if c == last:
+                rounded[1] = sb.tile([P, HALF * PACK], BF16, name="rounded1", align_bytes=64)
+                nc.scalar.activation(woven_order(rounded[1][:, CHUNK * PACK :])[:, 0], row_order(shifted[:])[:, 0], EXP)
+            nc.scalar.activation(y[:, c], shifted[:, 0], EXP)
+            nc.sync.dma_start(y_rows[:, :, cols], y[:, c])
 
-        rounded = []
-
-        def weave(c, copy, tag):
-            rounded.append(sb.tile([P, CHUNK * PACK], BF16, name=f"rounded{c}", tag=tag, align_bytes=64))
-            copy(
-                rounded[c][:].rearrange("p (a i t) -> p a t i", i=4, t=PACK),
-                y[c][:].rearrange("p t (a i) -> p a t i", i=4),
-            )
-
-        def quantise(c):
-            cols = slice(c * CHUNK, (c + 1) * CHUNK)
-            nc.vector.quantize_mx(y_codes[:, cols].bitcast(FP8X4), y_scales[:, cols], rounded[c][:])
+        def quantise(h):
+            cols = slice(h * HALF, (h + 1) * HALF)
+            nc.vector.quantize_mx(y_codes[:, cols].bitcast(FP8X4), y_scales[:, cols], rounded[h][:])
+            nc.sync.dma_start(words_out[:, cols], y_codes[:, cols])
 
         for c in range(chunks):
             scores(c)
-        weave(0, nc.vector.tensor_copy, "after_weave")
-        weave(1, nc.vector.tensor_copy, "rounded1")
+        rounded[0] = sb.tile([P, HALF * PACK], BF16, name="rounded0", tag="after_weave", align_bytes=64)
+        nc.vector.tensor_copy(woven_order(rounded[0][:]), row_order(y[:, 0:2]))
+        nc.vector.tensor_copy(woven_order(rounded[1][:, : CHUNK * PACK]), row_order(y[:, 2:3]))
         quantise(0)
-        weave(2, nc.vector.tensor_copy, "rounded2")
         quantise(1)
-        weave(3, nc.scalar.copy, "rounded3")
-        quantise(2)
-        nc.sync.dma_start(words_out[:, : 3 * CHUNK], y_codes[:, : 3 * CHUNK])
-        quantise(3)
-        nc.sync.dma_start(words_out[:, 3 * CHUNK :], y_codes[:, 3 * CHUNK :])
-        for g in range(4):
-            queue = nc.sync if g % 2 else nc.scalar
-            queue.dma_start(
-                out_2[0, 4 * g : 4 * g + 4, :].bitcast(I32),
-                y_scales[32 * g : 32 * g + 4, :].bitcast(I32),
-            )
+        scale_rows = out_2[0].rearrange("(g j) q -> j g q", j=4)
+        for j in range(4):
+            queue = nc.sync if j % 2 else nc.scalar
+            queue.dma_start(scale_rows[j].bitcast(I32), y_scales[j:P:32, :].bitcast(I32))

@@ -23,8 +23,9 @@ NQ = 512
 N = 512
 HALF = NQ // 2
 CHUNK = 128
+ON_SCALAR = (340, 170)
 CAST_COLS = POOL_Q // 2
-ON_SCALAR = (320, 160)
+ROW0 = P - 16
 
 FLOPS = 2 * D * N * NQ
 
@@ -38,51 +39,27 @@ def tile_attend_plw_lq_topk_kernel(tc, qT, k_words, k_scales, ls, offq, offs, ou
         q_rows = qT.rearrange("(p t) c -> p t c", t=PACK)
         raw = {}
 
-        def load_q(u, h):
-            raw[u, h] = sb.tile([P, 2, CAST_COLS], F32, name=f"raw{u}{h}")
-            nc.sync.dma_start(raw[u, h][:], q_rows[:, 2 * u : 2 * u + 2, h * CAST_COLS : (h + 1) * CAST_COLS])
+        def load_q(u, a, b):
+            raw[u, a] = sb.tile([P, 2, b - a], F32, name=f"raw{u}_{a}")
+            nc.sync.dma_start(raw[u, a][:], q_rows[:, 2 * u : 2 * u + 2, a:b])
 
         scale_pool = sb.tile([P, POOL_K], U8, name="scale_pool")
-        nc.gpsimd.memset(scale_pool[:].bitcast(I32), 0)
+        nc.gpsimd.memset(scale_pool[:ROW0, :].bitcast(I32), 0)
         k_list = sb.tile([P, N // 16], U16, name="k_list")
         nc.sync.dma_start(k_list[:], offs)
-        load_q(0, 0)
+        nc.scalar.dma_start(scale_pool[ROW0:, :].bitcast(I32), k_scales[0].bitcast(I32))
+        ls_cols = sb.tile([P, PACK], F32, name="ls_cols")
+        nc.scalar.dma_start(ls_cols[:], ls.rearrange("a b (p c) -> p (a b c)", c=PACK))
+        load_q(0, 0, POOL_Q)
         q_list = sb.tile([P, NQ // 16], U16, name="q_list")
         nc.sync.dma_start(q_list[:], offq)
-        nc.sync.dma_start(scale_pool[0:P:8, :].bitcast(I32), k_scales[0].bitcast(I32))
-        load_q(0, 1)
-        load_q(1, 0)
-        load_q(1, 1)
-        ls_cols = sb.tile([P, PACK], F32, name="ls_cols")
-        nc.sync.dma_start(ls_cols[:], ls.rearrange("a b (p c) -> p (a b c)", c=PACK))
+        load_q(1, 0, CAST_COLS)
+        load_q(1, CAST_COLS, POOL_Q)
         key_pool = sb.tile([P, POOL_K], I32, name="key_pool", tag="after_keys", align_bytes=64)
         nc.sync.dma_start(key_pool[:], k_words[0].rearrange("p n t -> p (n t)").bitcast(I32))
 
         ident = sb.tile([P, P], F32, name="ident")
         make_identity(nc, ident[:])
-
-        pairs = [sb.tile([P, POOL_Q, 2], BF16, name=f"pairs{u}") for u in range(2)]
-
-        def cast_scalar(u, h, a, b):
-            nc.scalar.activation(
-                pairs[u][:, h * CAST_COLS + a : h * CAST_COLS + b, :],
-                raw[u, h][:, :, a:b].rearrange("p t c -> p c t"),
-                COPY,
-            )
-
-        def cast_shared(u):
-            split = ON_SCALAR[u]
-            cast_scalar(u, 1, 0, split)
-            nc.vector.tensor_copy(
-                pairs[u][:, CAST_COLS + split :, :],
-                raw[u, 1][:, :, split:].rearrange("p t c -> p c t"),
-            )
-
-        cast_scalar(0, 0, 0, CAST_COLS)
-
-        ls_bank = ps.tile([P, PACK, P], F32, name="ls_bank")
-        for c in range(PACK):
-            nc.tensor.transpose(ls_bank[:, c, :], ls_cols[:, c : c + 1].to_broadcast([P, P]), ident[:])
 
         ks_listed = sb.tile([P, N], U8, name="ks_listed")
         nc.vector.tensor_copy(ks_listed[:], scale_pool[:].indirect(k_list[:]))
@@ -91,20 +68,40 @@ def tile_attend_plw_lq_topk_kernel(tc, qT, k_words, k_scales, ls, offq, offs, ou
             ks_dealt[:].rearrange("p (r s) -> p s r", r=PACK),
             ks_listed[:].rearrange("p (s r) -> p s r", r=PACK),
         )
+        for g in range(4):
+            nc.sync.dma_start(
+                ks_dealt[32 * g : 32 * g + 4, :].bitcast(I32), ks_dealt[ROW0 + 4 * g : ROW0 + 4 * g + 4, :].bitcast(I32)
+            )
 
-        for j in range(1, 4):
-            nc.sync.dma_start(ks_dealt[j:P:32, :].bitcast(I32), ks_dealt[8 * j : P : 32, :].bitcast(I32))
+        pairs = [sb.tile([P, POOL_Q, 2], BF16, name=f"pairs{u}") for u in range(2)]
 
-        listed = sb.tile([P, 2, NQ], U32, name="listed", tag="after_weave", align_bytes=64)
+        def cast(u, a, split):
+            width = raw[u, a].shape[2]
+            nc.scalar.activation(
+                pairs[u][:, a : a + split, :], raw[u, a][:, :, :split].rearrange("p t c -> p c t"), COPY
+            )
+            if split < width:
+                nc.vector.tensor_copy(
+                    pairs[u][:, a + split : a + width, :], raw[u, a][:, :, split:].rearrange("p t c -> p c t")
+                )
+
+        listed = sb.tile([P, 2, NQ], U32, name="listed")
 
         def gather_q(u, a, b):
             window = pairs[u][:].rearrange("p c t -> p (c t)").bitcast(U32)
             nc.vector.tensor_copy(listed[:, u, a:b], window.indirect(q_list[:, a // 16 : b // 16]))
 
-        cast_shared(0)
+        ls_bank = ps.tile([P, PACK, P], F32, name="ls_bank")
+        for c in range(PACK):
+            nc.tensor.transpose(ls_bank[:, c, :], ls_cols[:, c : c + 1].to_broadcast([P, P]), ident[:])
+        ls_rows = sb.tile([P, NQ], F32, name="ls_rows", tag="after_subs", align_bytes=64)
+        nc.scalar.copy(ls_rows[:].rearrange("p (n c) -> p n c", c=PACK), ls_bank[:].rearrange("p c n -> p n c"))
+
+        cast(0, 0, ON_SCALAR[0])
         gather_q(0, 0, NQ)
-        cast_scalar(1, 0, 0, CAST_COLS)
-        cast_shared(1)
+
+        cast(1, 0, CAST_COLS)
+        cast(1, CAST_COLS, ON_SCALAR[1])
         gather_q(1, 0, CHUNK)
         gather_q(1, CHUNK, NQ)
 
@@ -114,8 +111,6 @@ def tile_attend_plw_lq_topk_kernel(tc, qT, k_words, k_scales, ls, offq, offs, ou
                 woven[:, a * PACK : b * PACK].bitcast(U32).rearrange("p (c u) -> p c u", u=2),
                 listed[:, :, a:b].rearrange("p u c -> p c u"),
             )
-        ls_rows = sb.tile([P, NQ], F32, name="ls_rows", tag="after_weave", align_bytes=64)
-        nc.scalar.copy(ls_rows[:].rearrange("p (n c) -> p n c", c=PACK), ls_bank[:].rearrange("p c n -> p n c"))
 
         q_scales = sb.tile([P, NQ], U8, name="q_scales", align_bytes=64)
         first_codes = sb.tile([P, CHUNK], U32, name="first_codes", align_bytes=64)
@@ -135,24 +130,26 @@ def tile_attend_plw_lq_topk_kernel(tc, qT, k_words, k_scales, ls, offq, offs, ou
         y_scales = sb.tile([P, NQ], U8, name="y_scales", align_bytes=64)
         y_rows = out_0.rearrange("(s r) q -> s r q", r=PACK)
         words_out = out_1[0].rearrange("p q t -> p (q t)").bitcast(I32)
-        chunks = NQ // CHUNK
-        last = chunks - 1
-        y = sb.tile([P, chunks, PACK, CHUNK], F32, name="y")
-        rounded = {}
 
         def woven_order(tile):
-            return tile.rearrange("p (c a i t) -> p c a t i", a=CHUNK // 4, i=4, t=PACK)
+            return tile.rearrange("p (a i t) -> p a t i", i=4, t=PACK)
 
         def row_order(tile):
-            return tile.rearrange("p c t (a i) -> p c a t i", i=4)
+            return tile.rearrange("p t (a i) -> p a t i", i=4)
 
-        def scores(c):
-            bank = ps.tile([P, PACK, CHUNK], F32, name=f"bank{c}")
+        chunks = NQ // CHUNK
+        y = [sb.tile([P, PACK, CHUNK], F32, name=f"y{c}") for c in range(chunks)]
+        shifted = [sb.tile([P, PACK, CHUNK], F32, name=f"shifted{c}") for c in range(chunks)]
+
+        def scores(c, rows):
             cols = slice(c * CHUNK, (c + 1) * CHUNK)
+            count = rows.stop - rows.start
             q_codes = later_codes[:, (c - 1) * CHUNK : c * CHUNK] if c else first_codes[:]
-            for r in range(PACK):
+            bank = ps.tile([P, count, CHUNK], F32, name=f"bank{c}_{rows.start}")
+            for j in range(count):
+                r = rows.start + j
                 nc.tensor.matmul_mx(
-                    bank[:, r, :],
+                    bank[:, j, :],
                     lhsT=kw_dealt[:, r * P : (r + 1) * P].bitcast(FP8X4),
                     lhsT_scale=ks_dealt[:, r * P : (r + 1) * P],
                     rhs=q_codes.bitcast(FP8X4),
@@ -160,26 +157,33 @@ def tile_attend_plw_lq_topk_kernel(tc, qT, k_words, k_scales, ls, offq, offs, ou
                     start=True,
                     stop=True,
                 )
-            shifted = sb.tile([P, 1, PACK, CHUNK], F32, name=f"shifted{c}")
-            nc.vector.tensor_tensor(shifted[:, 0], bank[:], ls_rows[:, cols].unsqueeze(1).to_broadcast([P, PACK, CHUNK]), SUB)
-            if c == last:
-                rounded[1] = sb.tile([P, HALF * PACK], BF16, name="rounded1", align_bytes=64)
-                nc.scalar.activation(woven_order(rounded[1][:, CHUNK * PACK :])[:, 0], row_order(shifted[:])[:, 0], EXP)
-            nc.scalar.activation(y[:, c], shifted[:, 0], EXP)
-            nc.sync.dma_start(y_rows[:, :, cols], y[:, c])
+            nc.vector.tensor_tensor(
+                shifted[c][:, rows, :], bank[:], ls_rows[:, cols].unsqueeze(1).to_broadcast([P, count, CHUNK]), SUB
+            )
 
-        def quantise(h):
-            cols = slice(h * HALF, (h + 1) * HALF)
-            nc.vector.quantize_mx(y_codes[:, cols].bitcast(FP8X4), y_scales[:, cols], rounded[h][:])
-            nc.sync.dma_start(words_out[:, cols], y_codes[:, cols])
+        def weights(c, rows):
+            nc.scalar.activation(y[c][:, rows, :], shifted[c][:, rows, :], EXP)
+            nc.sync.dma_start(y_rows[:, rows, c * CHUNK : (c + 1) * CHUNK], y[c][:, rows, :])
 
-        for c in range(chunks):
-            scores(c)
-        rounded[0] = sb.tile([P, HALF * PACK], BF16, name="rounded0", tag="after_weave", align_bytes=64)
-        nc.vector.tensor_copy(woven_order(rounded[0][:]), row_order(y[:, 0:2]))
-        nc.vector.tensor_copy(woven_order(rounded[1][:, : CHUNK * PACK]), row_order(y[:, 2:3]))
-        quantise(0)
-        quantise(1)
+        def quantise(a, b, tile):
+            nc.vector.quantize_mx(y_codes[:, a:b].bitcast(FP8X4), y_scales[:, a:b], tile)
+            nc.sync.dma_start(words_out[:, a:b], y_codes[:, a:b])
+
+        for rows in (slice(0, 2), slice(2, 4)):
+            scores(0, rows)
+            weights(0, rows)
+        for c in (1, 2):
+            scores(c, slice(0, 4))
+            weights(c, slice(0, 4))
+        for rows in (slice(0, 2), slice(2, 4)):
+            scores(3, rows)
+        rounded = sb.tile([P, chunks, CHUNK * PACK], BF16, name="rounded", tag="after_subs", align_bytes=64)
+        nc.scalar.activation(woven_order(rounded[:, 3]), row_order(shifted[3][:]), EXP)
+        weights(3, slice(0, 4))
+        for c in range(3):
+            nc.vector.tensor_copy(woven_order(rounded[:, c]), row_order(y[c][:]))
+        for h in range(2):
+            quantise(h * HALF, (h + 1) * HALF, rounded[:, 2 * h : 2 * h + 2].rearrange("p c x -> p (c x)"))
         scale_rows = out_2[0].rearrange("(g j) q -> j g q", j=4)
         for j in range(4):
             queue = nc.sync if j % 2 else nc.scalar

@@ -13,6 +13,8 @@ FP8X4 = mybir.dt.float8_e4m3fn_x4
 COPY = mybir.ActivationFunctionType.Copy
 EXP = mybir.ActivationFunctionType.Exp
 SUB = mybir.AluOpType.subtract
+MULT = mybir.AluOpType.mult
+ADD = mybir.AluOpType.add
 
 P = 128
 PACK = 4
@@ -47,9 +49,9 @@ def tile_attend_plw_lq_topk_kernel(tc, qT, k_words, k_scales, ls, offq, offs, ou
         nc.gpsimd.memset(scale_pool[:ROW0, :].bitcast(I32), 0)
         k_list = sb.tile([P, N // 16], U16, name="k_list")
         nc.sync.dma_start(k_list[:], offs)
-        nc.scalar.dma_start(scale_pool[ROW0:, :].bitcast(I32), k_scales[0].bitcast(I32))
+        nc.sync.dma_start(scale_pool[ROW0:, :].bitcast(I32), k_scales[0].bitcast(I32))
         ls_cols = sb.tile([P, PACK], F32, name="ls_cols")
-        nc.scalar.dma_start(ls_cols[:], ls.rearrange("a b (p c) -> p (a b c)", c=PACK))
+        nc.sync.dma_start(ls_cols[:], ls.rearrange("a b (p c) -> p (a b c)", c=PACK))
         load_q(0, 0, POOL_Q)
         q_list = sb.tile([P, NQ // 16], U16, name="q_list")
         nc.sync.dma_start(q_list[:], offq)
@@ -65,8 +67,8 @@ def tile_attend_plw_lq_topk_kernel(tc, qT, k_words, k_scales, ls, offq, offs, ou
         nc.vector.tensor_copy(ks_listed[:], scale_pool[:].indirect(k_list[:]))
         ks_dealt = sb.tile([P, N], U8, name="ks_dealt", align_bytes=64)
         nc.vector.tensor_copy(
-            ks_dealt[:].rearrange("p (r s) -> p s r", r=PACK),
-            ks_listed[:].rearrange("p (s r) -> p s r", r=PACK),
+            ks_dealt[:].rearrange("p (r s) -> p r s", r=PACK),
+            ks_listed[:].rearrange("p (s r) -> p r s", r=PACK),
         )
         for g in range(4):
             nc.sync.dma_start(
@@ -94,7 +96,7 @@ def tile_attend_plw_lq_topk_kernel(tc, qT, k_words, k_scales, ls, offq, offs, ou
         ls_bank = ps.tile([P, PACK, P], F32, name="ls_bank")
         for c in range(PACK):
             nc.tensor.transpose(ls_bank[:, c, :], ls_cols[:, c : c + 1].to_broadcast([P, P]), ident[:])
-        ls_rows = sb.tile([P, NQ], F32, name="ls_rows", tag="after_subs", align_bytes=64)
+        ls_rows = sb.tile([P, NQ], F32, name="ls_rows")
         nc.scalar.copy(ls_rows[:].rearrange("p (n c) -> p n c", c=PACK), ls_bank[:].rearrange("p c n -> p n c"))
 
         cast(0, 0, ON_SCALAR[0])
@@ -169,18 +171,21 @@ def tile_attend_plw_lq_topk_kernel(tc, qT, k_words, k_scales, ls, offq, offs, ou
             nc.vector.quantize_mx(y_codes[:, a:b].bitcast(FP8X4), y_scales[:, a:b], tile)
             nc.sync.dma_start(words_out[:, a:b], y_codes[:, a:b])
 
+        rounded = sb.tile([P, chunks, CHUNK * PACK], BF16, name="rounded", align_bytes=64)
         for rows in (slice(0, 2), slice(2, 4)):
             scores(0, rows)
             weights(0, rows)
+        nc.gpsimd.tensor_scalar(
+            rounded[:, 0].rearrange("p (c t) -> p c t", t=PACK), y[0][:].rearrange("p t c -> p c t"), 1.0, 0.0, MULT, ADD
+        )
         for c in (1, 2):
             scores(c, slice(0, 4))
             weights(c, slice(0, 4))
         for rows in (slice(0, 2), slice(2, 4)):
             scores(3, rows)
-        rounded = sb.tile([P, chunks, CHUNK * PACK], BF16, name="rounded", tag="after_subs", align_bytes=64)
         nc.scalar.activation(woven_order(rounded[:, 3]), row_order(shifted[3][:]), EXP)
         weights(3, slice(0, 4))
-        for c in range(3):
+        for c in (1, 2):
             nc.vector.tensor_copy(woven_order(rounded[:, c]), row_order(y[c][:]))
         for h in range(2):
             quantise(h * HALF, (h + 1) * HALF, rounded[:, 2 * h : 2 * h + 2].rearrange("p c x -> p (c x)"))

@@ -25,8 +25,8 @@ NQ = 512
 N = 512
 HALF = NQ // 2
 CHUNK = 128
-ON_SCALAR = (340, 170)
-CAST_COLS = POOL_Q // 2
+SPLIT = 768
+ON_SCALAR = (290, 96)
 ROW0 = P - 16
 
 FLOPS = 2 * D * N * NQ
@@ -50,15 +50,17 @@ def tile_attend_plw_lq_topk_kernel(tc, qT, k_words, k_scales, ls, offq, offs, ou
         k_list = sb.tile([P, N // 16], U16, name="k_list")
         nc.sync.dma_start(k_list[:], offs)
         nc.sync.dma_start(scale_pool[ROW0:, :].bitcast(I32), k_scales[0].bitcast(I32))
-        ls_cols = sb.tile([P, PACK], F32, name="ls_cols")
-        nc.sync.dma_start(ls_cols[:], ls.rearrange("a b (p c) -> p (a b c)", c=PACK))
-        load_q(0, 0, POOL_Q)
+        load_q(0, 0, SPLIT)
         q_list = sb.tile([P, NQ // 16], U16, name="q_list")
         nc.sync.dma_start(q_list[:], offq)
-        load_q(1, 0, CAST_COLS)
-        load_q(1, CAST_COLS, POOL_Q)
+        load_q(0, SPLIT, POOL_Q)
+        load_q(1, 0, SPLIT)
+        load_q(1, SPLIT, POOL_Q)
         key_pool = sb.tile([P, POOL_K], I32, name="key_pool", tag="after_keys", align_bytes=64)
         nc.sync.dma_start(key_pool[:], k_words[0].rearrange("p n t -> p (n t)").bitcast(I32))
+
+        ls_cols = sb.tile([P, PACK], F32, name="ls_cols")
+        nc.sync.dma_start(ls_cols[:], ls.rearrange("a b (p c) -> p (a b c)", c=PACK))
 
         ident = sb.tile([P, P], F32, name="ident")
         make_identity(nc, ident[:])
@@ -93,17 +95,12 @@ def tile_attend_plw_lq_topk_kernel(tc, qT, k_words, k_scales, ls, offq, offs, ou
             window = pairs[u][:].rearrange("p c t -> p (c t)").bitcast(U32)
             nc.vector.tensor_copy(listed[:, u, a:b], window.indirect(q_list[:, a // 16 : b // 16]))
 
-        ls_bank = ps.tile([P, PACK, P], F32, name="ls_bank")
-        for c in range(PACK):
-            nc.tensor.transpose(ls_bank[:, c, :], ls_cols[:, c : c + 1].to_broadcast([P, P]), ident[:])
-        ls_rows = sb.tile([P, NQ], F32, name="ls_rows")
-        nc.scalar.copy(ls_rows[:].rearrange("p (n c) -> p n c", c=PACK), ls_bank[:].rearrange("p c n -> p n c"))
-
         cast(0, 0, ON_SCALAR[0])
+        cast(0, SPLIT, ON_SCALAR[1])
         gather_q(0, 0, NQ)
 
-        cast(1, 0, CAST_COLS)
-        cast(1, CAST_COLS, ON_SCALAR[1])
+        cast(1, 0, ON_SCALAR[0])
+        cast(1, SPLIT, ON_SCALAR[1])
         gather_q(1, 0, CHUNK)
         gather_q(1, CHUNK, NQ)
 
@@ -112,6 +109,16 @@ def tile_attend_plw_lq_topk_kernel(tc, qT, k_words, k_scales, ls, offq, offs, ou
             nc.scalar.copy(
                 woven[:, a * PACK : b * PACK].bitcast(U32).rearrange("p (c u) -> p c u", u=2),
                 listed[:, :, a:b].rearrange("p u c -> p c u"),
+            )
+
+        ls_bank = ps.tile([P, PACK, P], F32, name="ls_bank")
+        for c in range(PACK):
+            nc.tensor.transpose(ls_bank[:, c, :], ls_cols[:, c : c + 1].to_broadcast([P, P]), ident[:])
+        ls_rows = sb.tile([P, NQ], F32, name="ls_rows")
+        for a, b in ((0, CHUNK), (CHUNK, NQ)):
+            nc.scalar.copy(
+                ls_rows[:, a:b].rearrange("p (n c) -> p n c", c=PACK),
+                ls_bank[:, :, a // PACK : b // PACK].rearrange("p c n -> p n c"),
             )
 
         q_scales = sb.tile([P, NQ], U8, name="q_scales", align_bytes=64)

@@ -114,7 +114,7 @@ def tile_attend_plw_lq_topk_kernel(tc, qT, k_words, k_scales, ls, offq, offs, ou
         ls_bank = ps.tile([P, PACK, P], F32, name="ls_bank")
         for c in range(PACK):
             nc.tensor.transpose(ls_bank[:, c, :], ls_cols[:, c : c + 1].to_broadcast([P, P]), ident[:])
-        ls_rows = sb.tile([P, NQ], F32, name="ls_rows")
+        ls_rows = sb.tile([P, NQ], F32, name="ls_rows", tag="after_subs", align_bytes=64)
         for a, b in ((0, CHUNK), (CHUNK, NQ)):
             nc.scalar.copy(
                 ls_rows[:, a:b].rearrange("p (n c) -> p n c", c=PACK),
@@ -146,56 +146,70 @@ def tile_attend_plw_lq_topk_kernel(tc, qT, k_words, k_scales, ls, offq, offs, ou
         def row_order(tile):
             return tile.rearrange("p t (a i) -> p a t i", i=4)
 
-        chunks = NQ // CHUNK
-        y = [sb.tile([P, PACK, CHUNK], F32, name=f"y{c}") for c in range(chunks)]
-        shifted = [sb.tile([P, PACK, CHUNK], F32, name=f"shifted{c}") for c in range(chunks)]
+        y = [sb.tile([P, PACK, HALF], F32, name=f"y{h}") for h in range(2)]
+        shifted = [sb.tile([P, PACK, HALF], F32, name=f"shifted{h}") for h in range(2)]
 
-        def scores(c, rows):
-            cols = slice(c * CHUNK, (c + 1) * CHUNK)
-            count = rows.stop - rows.start
-            q_codes = later_codes[:, (c - 1) * CHUNK : c * CHUNK] if c else first_codes[:]
-            bank = ps.tile([P, count, CHUNK], F32, name=f"bank{c}_{rows.start}")
-            for j in range(count):
-                r = rows.start + j
-                nc.tensor.matmul_mx(
-                    bank[:, j, :],
-                    lhsT=kw_dealt[:, r * P : (r + 1) * P].bitcast(FP8X4),
-                    lhsT_scale=ks_dealt[:, r * P : (r + 1) * P],
-                    rhs=q_codes.bitcast(FP8X4),
-                    rhs_scale=q_scales[:, cols],
-                    start=True,
-                    stop=True,
-                )
+        def codes(a, b):
+            return later_codes[:, a - CHUNK : b - CHUNK] if a else first_codes[:]
+
+        def scores(r0, a, b, width):
+            h, o = divmod(a, HALF)
+            bank = ps.tile([P, 2, b - a], F32, name=f"bank{r0}_{a}")
+            for j in range(2):
+                r = r0 + j
+                for c in range(a, b, width):
+                    nc.tensor.matmul_mx(
+                        bank[:, j, c - a : c - a + width],
+                        lhsT=kw_dealt[:, r * P : (r + 1) * P].bitcast(FP8X4),
+                        lhsT_scale=ks_dealt[:, r * P : (r + 1) * P],
+                        rhs=codes(c, c + width).bitcast(FP8X4),
+                        rhs_scale=q_scales[:, c : c + width],
+                        start=True,
+                        stop=True,
+                    )
             nc.vector.tensor_tensor(
-                shifted[c][:, rows, :], bank[:], ls_rows[:, cols].unsqueeze(1).to_broadcast([P, count, CHUNK]), SUB
+                shifted[h][:, r0 : r0 + 2, o : o + b - a],
+                bank[:],
+                ls_rows[:, a:b].unsqueeze(1).to_broadcast([P, 2, b - a]),
+                SUB,
             )
+            nc.scalar.activation(y[h][:, r0 : r0 + 2, o : o + b - a], shifted[h][:, r0 : r0 + 2, o : o + b - a], EXP)
 
-        def weights(c, rows):
-            nc.scalar.activation(y[c][:, rows, :], shifted[c][:, rows, :], EXP)
-            nc.sync.dma_start(y_rows[:, rows, c * CHUNK : (c + 1) * CHUNK], y[c][:, rows, :])
+        def store(r0, h):
+            nc.sync.dma_start(y_rows[:, r0 : r0 + 2, h * HALF : (h + 1) * HALF], y[h][:, r0 : r0 + 2, :])
 
         def quantise(a, b, tile):
             nc.vector.quantize_mx(y_codes[:, a:b].bitcast(FP8X4), y_scales[:, a:b], tile)
-            nc.sync.dma_start(words_out[:, a:b], y_codes[:, a:b])
 
-        rounded = sb.tile([P, chunks, CHUNK * PACK], BF16, name="rounded", align_bytes=64)
-        for rows in (slice(0, 2), slice(2, 4)):
-            scores(0, rows)
-            weights(0, rows)
+        first_rounded = sb.tile([P, CHUNK * PACK], BF16, name="first_rounded", align_bytes=64)
+        for r0 in (0, 2):
+            scores(r0, 0, CHUNK, CHUNK)
         nc.gpsimd.tensor_scalar(
-            rounded[:, 0].rearrange("p (c t) -> p c t", t=PACK), y[0][:].rearrange("p t c -> p c t"), 1.0, 0.0, MULT, ADD
+            first_rounded[:].rearrange("p (c t) -> p c t", t=PACK),
+            y[0][:, :, :CHUNK].rearrange("p t c -> p c t"),
+            1.0,
+            0.0,
+            MULT,
+            ADD,
         )
-        for c in (1, 2):
-            scores(c, slice(0, 4))
-            weights(c, slice(0, 4))
-        for rows in (slice(0, 2), slice(2, 4)):
-            scores(3, rows)
-        nc.scalar.activation(woven_order(rounded[:, 3]), row_order(shifted[3][:]), EXP)
-        weights(3, slice(0, 4))
-        for c in (1, 2):
-            nc.vector.tensor_copy(woven_order(rounded[:, c]), row_order(y[c][:]))
-        for h in range(2):
-            quantise(h * HALF, (h + 1) * HALF, rounded[:, 2 * h : 2 * h + 2].rearrange("p c x -> p (c x)"))
+        for r0 in (0, 2):
+            scores(r0, CHUNK, HALF, CHUNK)
+            store(r0, 0)
+        scores(0, HALF, NQ, HALF)
+        store(0, 1)
+        for a in (HALF, NQ - CHUNK):
+            scores(2, a, a + CHUNK, CHUNK)
+        store(2, 1)
+        rounded = sb.tile([P, (NQ - CHUNK) * PACK], BF16, name="rounded", tag="after_subs", align_bytes=64)
+        woven_y = [first_rounded[:]] + [rounded[:, c * CHUNK * PACK : (c + 1) * CHUNK * PACK] for c in range(3)]
+        nc.scalar.activation(woven_order(woven_y[3]), row_order(shifted[1][:, :, CHUNK:]), EXP)
+        nc.vector.tensor_copy(woven_order(woven_y[1]), row_order(y[0][:, :, CHUNK:]))
+        nc.vector.tensor_copy(woven_order(woven_y[2]), row_order(y[1][:, :, :CHUNK]))
+        quantise(0, CHUNK, woven_y[0])
+        quantise(CHUNK, NQ - CHUNK, rounded[:, : HALF * PACK])
+        nc.sync.dma_start(words_out[:, : NQ - CHUNK], y_codes[:, : NQ - CHUNK])
+        quantise(NQ - CHUNK, NQ, woven_y[3])
+        nc.sync.dma_start(words_out[:, NQ - CHUNK :], y_codes[:, NQ - CHUNK :])
         scale_rows = out_2[0].rearrange("(g j) q -> j g q", j=4)
         for j in range(4):
             queue = nc.sync if j % 2 else nc.scalar

@@ -26,7 +26,7 @@ N = 512
 HALF = NQ // 2
 CHUNK = 128
 SPLIT = 768
-ON_SCALAR = (290, 96)
+ON_SCALAR = ((288, 96), (352, 72))
 ROW0 = P - 16
 
 FLOPS = 2 * D * N * NQ
@@ -49,7 +49,7 @@ def tile_attend_plw_lq_topk_kernel(tc, qT, k_words, k_scales, ls, offq, offs, ou
         nc.gpsimd.memset(scale_pool[:ROW0, :].bitcast(I32), 0)
         k_list = sb.tile([P, N // 16], U16, name="k_list")
         nc.sync.dma_start(k_list[:], offs)
-        nc.sync.dma_start(scale_pool[ROW0:, :].bitcast(I32), k_scales[0].bitcast(I32))
+        nc.scalar.dma_start(scale_pool[ROW0:, :].bitcast(I32), k_scales[0].bitcast(I32))
         load_q(0, 0, SPLIT)
         q_list = sb.tile([P, NQ // 16], U16, name="q_list")
         nc.sync.dma_start(q_list[:], offq)
@@ -95,12 +95,12 @@ def tile_attend_plw_lq_topk_kernel(tc, qT, k_words, k_scales, ls, offq, offs, ou
             window = pairs[u][:].rearrange("p c t -> p (c t)").bitcast(U32)
             nc.vector.tensor_copy(listed[:, u, a:b], window.indirect(q_list[:, a // 16 : b // 16]))
 
-        cast(0, 0, ON_SCALAR[0])
-        cast(0, SPLIT, ON_SCALAR[1])
+        cast(0, 0, ON_SCALAR[0][0])
+        cast(0, SPLIT, ON_SCALAR[0][1])
         gather_q(0, 0, NQ)
 
-        cast(1, 0, ON_SCALAR[0])
-        cast(1, SPLIT, ON_SCALAR[1])
+        cast(1, 0, ON_SCALAR[1][0])
+        cast(1, SPLIT, ON_SCALAR[1][1])
         gather_q(1, 0, CHUNK)
         gather_q(1, CHUNK, NQ)
 

@@ -56,7 +56,7 @@ def tile_attend_plw_lq_topk_kernel(tc, qT, k_words, k_scales, ls, offq, offs, ou
         load_q(0, SPLIT, POOL_Q)
         load_q(1, 0, SPLIT)
         load_q(1, SPLIT, POOL_Q)
-        key_pool = sb.tile([P, POOL_K], I32, name="key_pool", tag="after_keys", align_bytes=64)
+        key_pool = sb.tile([P, POOL_K], I32, name="key_pool")
         nc.sync.dma_start(key_pool[:], k_words[0].rearrange("p n t -> p (n t)").bitcast(I32))
 
         ls_cols = sb.tile([P, PACK], F32, name="ls_cols")
@@ -68,13 +68,15 @@ def tile_attend_plw_lq_topk_kernel(tc, qT, k_words, k_scales, ls, offq, offs, ou
         ks_listed = sb.tile([P, N], U8, name="ks_listed")
         nc.vector.tensor_copy(ks_listed[:], scale_pool[:].indirect(k_list[:]))
         ks_dealt = sb.tile([P, N], U8, name="ks_dealt", align_bytes=64)
+        nc.gpsimd.memset(ks_dealt[:].bitcast(I32), 0)
+        ks_rows = sb.tile([P, N], U8, name="ks_rows", tag="after_moves", align_bytes=64)
         nc.vector.tensor_copy(
-            ks_dealt[:].rearrange("p (r s) -> p r s", r=PACK),
+            ks_rows[:].rearrange("p (r s) -> p r s", r=PACK),
             ks_listed[:].rearrange("p (s r) -> p r s", r=PACK),
         )
         for g in range(4):
             nc.sync.dma_start(
-                ks_dealt[32 * g : 32 * g + 4, :].bitcast(I32), ks_dealt[ROW0 + 4 * g : ROW0 + 4 * g + 4, :].bitcast(I32)
+                ks_dealt[32 * g : 32 * g + 4, :].bitcast(I32), ks_rows[ROW0 + 4 * g : ROW0 + 4 * g + 4, :].bitcast(I32)
             )
 
         pairs = [sb.tile([P, POOL_Q, 2], BF16, name=f"pairs{u}") for u in range(2)]
@@ -111,10 +113,10 @@ def tile_attend_plw_lq_topk_kernel(tc, qT, k_words, k_scales, ls, offq, offs, ou
                 listed[:, :, a:b].rearrange("p u c -> p c u"),
             )
 
-        ls_bank = ps.tile([P, PACK, P], F32, name="ls_bank")
+        ls_bank = ps.tile([P, PACK, P], F32, name="ls_bank", tag="ls_then_last")
         for c in range(PACK):
             nc.tensor.transpose(ls_bank[:, c, :], ls_cols[:, c : c + 1].to_broadcast([P, P]), ident[:])
-        ls_rows = sb.tile([P, NQ], F32, name="ls_rows", tag="after_subs", align_bytes=64)
+        ls_rows = sb.tile([P, NQ], F32, name="ls_rows")
         for a, b in ((0, CHUNK), (CHUNK, NQ)):
             nc.scalar.copy(
                 ls_rows[:, a:b].rearrange("p (n c) -> p n c", c=PACK),
@@ -124,12 +126,12 @@ def tile_attend_plw_lq_topk_kernel(tc, qT, k_words, k_scales, ls, offq, offs, ou
         q_scales = sb.tile([P, NQ], U8, name="q_scales", align_bytes=64)
         first_codes = sb.tile([P, CHUNK], U32, name="first_codes", align_bytes=64)
         nc.vector.quantize_mx(first_codes[:].bitcast(FP8X4), q_scales[:, :CHUNK], woven[:, : CHUNK * PACK])
-        kw_dealt = sb.tile([P, N], U32, name="kw_dealt", align_bytes=64)
+        kw_dealt = sb.tile([P, N], U32, name="kw_dealt", tag="after_passes", align_bytes=64)
         nc.vector.tensor_copy(
             kw_dealt[:].rearrange("p (r s) -> p s r", r=PACK),
             key_pool[:].bitcast(U32).indirect(k_list[:]),
         )
-        later_codes = sb.tile([P, NQ - CHUNK], U32, name="later_codes", tag="after_keys", align_bytes=64)
+        later_codes = sb.tile([P, NQ - CHUNK], U32, name="later_codes", tag="after_moves", align_bytes=64)
         for a, b in ((CHUNK, HALF), (HALF, NQ)):
             nc.vector.quantize_mx(
                 later_codes[:, a - CHUNK : b - CHUNK].bitcast(FP8X4), q_scales[:, a:b], woven[:, a * PACK : b * PACK]
@@ -152,14 +154,14 @@ def tile_attend_plw_lq_topk_kernel(tc, qT, k_words, k_scales, ls, offq, offs, ou
         def codes(a, b):
             return later_codes[:, a - CHUNK : b - CHUNK] if a else first_codes[:]
 
-        def scores(r0, a, b, width):
+        def scores(r0, r1, a, b, width, tag=None):
             h, o = divmod(a, HALF)
-            bank = ps.tile([P, 2, b - a], F32, name=f"bank{r0}_{a}")
-            for j in range(2):
-                r = r0 + j
+            name = f"bank{r0}_{a}"
+            bank = ps.tile([P, r1 - r0, b - a], F32, name=name, tag=tag or name)
+            for r in range(r0, r1):
                 for c in range(a, b, width):
                     nc.tensor.matmul_mx(
-                        bank[:, j, c - a : c - a + width],
+                        bank[:, r - r0, c - a : c - a + width],
                         lhsT=kw_dealt[:, r * P : (r + 1) * P].bitcast(FP8X4),
                         lhsT_scale=ks_dealt[:, r * P : (r + 1) * P],
                         rhs=codes(c, c + width).bitcast(FP8X4),
@@ -168,22 +170,22 @@ def tile_attend_plw_lq_topk_kernel(tc, qT, k_words, k_scales, ls, offq, offs, ou
                         stop=True,
                     )
             nc.vector.tensor_tensor(
-                shifted[h][:, r0 : r0 + 2, o : o + b - a],
+                shifted[h][:, r0:r1, o : o + b - a],
                 bank[:],
-                ls_rows[:, a:b].unsqueeze(1).to_broadcast([P, 2, b - a]),
+                ls_rows[:, a:b].unsqueeze(1).to_broadcast([P, r1 - r0, b - a]),
                 SUB,
             )
-            nc.scalar.activation(y[h][:, r0 : r0 + 2, o : o + b - a], shifted[h][:, r0 : r0 + 2, o : o + b - a], EXP)
+            nc.scalar.activation(y[h][:, r0:r1, o : o + b - a], shifted[h][:, r0:r1, o : o + b - a], EXP)
 
-        def store(r0, h):
-            nc.sync.dma_start(y_rows[:, r0 : r0 + 2, h * HALF : (h + 1) * HALF], y[h][:, r0 : r0 + 2, :])
+        def store(r0, r1, h):
+            nc.sync.dma_start(y_rows[:, r0:r1, h * HALF : (h + 1) * HALF], y[h][:, r0:r1, :])
 
         def quantise(a, b, tile):
             nc.vector.quantize_mx(y_codes[:, a:b].bitcast(FP8X4), y_scales[:, a:b], tile)
 
         first_rounded = sb.tile([P, CHUNK * PACK], BF16, name="first_rounded", align_bytes=64)
         for r0 in (0, 2):
-            scores(r0, 0, CHUNK, CHUNK)
+            scores(r0, r0 + 2, 0, CHUNK, CHUNK)
         nc.gpsimd.tensor_scalar(
             first_rounded[:].rearrange("p (c t) -> p c t", t=PACK),
             y[0][:, :, :CHUNK].rearrange("p t c -> p c t"),
@@ -193,14 +195,15 @@ def tile_attend_plw_lq_topk_kernel(tc, qT, k_words, k_scales, ls, offq, offs, ou
             ADD,
         )
         for r0 in (0, 2):
-            scores(r0, CHUNK, HALF, CHUNK)
-            store(r0, 0)
-        scores(0, HALF, NQ, HALF)
-        store(0, 1)
-        for a in (HALF, NQ - CHUNK):
-            scores(2, a, a + CHUNK, CHUNK)
-        store(2, 1)
-        rounded = sb.tile([P, (NQ - CHUNK) * PACK], BF16, name="rounded", tag="after_subs", align_bytes=64)
+            scores(r0, r0 + 2, CHUNK, HALF, CHUNK)
+            store(r0, r0 + 2, 0)
+        for r in (0, 1):
+            scores(r, r + 1, HALF, NQ, HALF)
+        store(0, 2, 1)
+        scores(2, 4, HALF, NQ - CHUNK, CHUNK)
+        scores(2, 4, NQ - CHUNK, NQ, CHUNK, tag="ls_then_last")
+        store(2, 4, 1)
+        rounded = sb.tile([P, (NQ - CHUNK) * PACK], BF16, name="rounded", tag="after_passes", align_bytes=64)
         woven_y = [first_rounded[:]] + [rounded[:, c * CHUNK * PACK : (c + 1) * CHUNK * PACK] for c in range(3)]
         nc.scalar.activation(woven_order(woven_y[3]), row_order(shifted[1][:, :, CHUNK:]), EXP)
         nc.vector.tensor_copy(woven_order(woven_y[1]), row_order(y[0][:, :, CHUNK:]))

@@ -13,8 +13,6 @@ FP8X4 = mybir.dt.float8_e4m3fn_x4
 COPY = mybir.ActivationFunctionType.Copy
 EXP = mybir.ActivationFunctionType.Exp
 SUB = mybir.AluOpType.subtract
-MULT = mybir.AluOpType.mult
-ADD = mybir.AluOpType.add
 
 P = 128
 PACK = 4
@@ -107,13 +105,13 @@ def tile_attend_plw_lq_topk_kernel(tc, qT, k_words, k_scales, ls, offq, offs, ou
         gather_q(1, CHUNK, NQ)
 
         woven = sb.tile([P, NQ * PACK], BF16, name="woven", align_bytes=64)
-        for a, b in ((0, CHUNK), (CHUNK, NQ)):
+        for a, b in ((0, CHUNK), (CHUNK, HALF), (HALF, NQ)):
             nc.scalar.copy(
                 woven[:, a * PACK : b * PACK].bitcast(U32).rearrange("p (c u) -> p c u", u=2),
                 listed[:, :, a:b].rearrange("p u c -> p c u"),
             )
 
-        ls_bank = ps.tile([P, PACK, P], F32, name="ls_bank", tag="ls_then_last")
+        ls_bank = ps.tile([P, PACK, P], F32, name="ls_bank")
         for c in range(PACK):
             nc.tensor.transpose(ls_bank[:, c, :], ls_cols[:, c : c + 1].to_broadcast([P, P]), ident[:])
         ls_rows = sb.tile([P, NQ], F32, name="ls_rows")
@@ -183,36 +181,29 @@ def tile_attend_plw_lq_topk_kernel(tc, qT, k_words, k_scales, ls, offq, offs, ou
         def quantise(a, b, tile):
             nc.vector.quantize_mx(y_codes[:, a:b].bitcast(FP8X4), y_scales[:, a:b], tile)
 
-        first_rounded = sb.tile([P, CHUNK * PACK], BF16, name="first_rounded", align_bytes=64)
-        for r0 in (0, 2):
-            scores(r0, r0 + 2, 0, CHUNK, CHUNK)
-        nc.gpsimd.tensor_scalar(
-            first_rounded[:].rearrange("p (c t) -> p c t", t=PACK),
-            y[0][:, :, :CHUNK].rearrange("p t c -> p c t"),
-            1.0,
-            0.0,
-            MULT,
-            ADD,
-        )
-        for r0 in (0, 2):
-            scores(r0, r0 + 2, CHUNK, HALF, CHUNK)
-            store(r0, r0 + 2, 0)
+        for c in (0, CHUNK):
+            scores(0, 2, c, c + CHUNK, CHUNK)
+        store(0, 2, 0)
         for r in (0, 1):
             scores(r, r + 1, HALF, NQ, HALF)
         store(0, 2, 1)
-        scores(2, 4, HALF, NQ - CHUNK, CHUNK)
-        scores(2, 4, NQ - CHUNK, NQ, CHUNK, tag="ls_then_last")
+        for c in (HALF, NQ - CHUNK):
+            scores(2, 4, c, c + CHUNK, CHUNK)
         store(2, 4, 1)
-        rounded = sb.tile([P, (NQ - CHUNK) * PACK], BF16, name="rounded", tag="after_passes", align_bytes=64)
-        woven_y = [first_rounded[:]] + [rounded[:, c * CHUNK * PACK : (c + 1) * CHUNK * PACK] for c in range(3)]
-        nc.scalar.activation(woven_order(woven_y[3]), row_order(shifted[1][:, :, CHUNK:]), EXP)
-        nc.vector.tensor_copy(woven_order(woven_y[1]), row_order(y[0][:, :, CHUNK:]))
-        nc.vector.tensor_copy(woven_order(woven_y[2]), row_order(y[1][:, :, :CHUNK]))
+        for c in (0, CHUNK):
+            scores(2, 4, c, c + CHUNK, CHUNK, tag=f"bank0_{c}")
+        store(2, 4, 0)
+        rounded = sb.tile([P, NQ * PACK], BF16, name="rounded", tag="after_passes", align_bytes=64)
+        woven_y = [rounded[:, c * CHUNK * PACK : (c + 1) * CHUNK * PACK] for c in range(4)]
+        nc.scalar.activation(woven_order(woven_y[1]), row_order(shifted[0][:, :, CHUNK:]), EXP)
+        for c in (2, 3, 0):
+            h, o = divmod(c * CHUNK, HALF)
+            nc.vector.tensor_copy(woven_order(woven_y[c]), row_order(y[h][:, :, o : o + CHUNK]))
+        quantise(HALF, NQ, rounded[:, HALF * PACK :])
+        nc.sync.dma_start(words_out[:, HALF:], y_codes[:, HALF:])
         quantise(0, CHUNK, woven_y[0])
-        quantise(CHUNK, NQ - CHUNK, rounded[:, : HALF * PACK])
-        nc.sync.dma_start(words_out[:, : NQ - CHUNK], y_codes[:, : NQ - CHUNK])
-        quantise(NQ - CHUNK, NQ, woven_y[3])
-        nc.sync.dma_start(words_out[:, NQ - CHUNK :], y_codes[:, NQ - CHUNK :])
+        quantise(CHUNK, HALF, woven_y[1])
+        nc.sync.dma_start(words_out[:, :HALF], y_codes[:, :HALF])
         scale_rows = out_2[0].rearrange("(g j) q -> j g q", j=4)
         for j in range(4):
             queue = nc.sync if j % 2 else nc.scalar

@@ -129,11 +129,10 @@ def tile_attend_plw_lq_topk_kernel(tc, qT, k_words, k_scales, ls, offq, offs, ou
             kw_dealt[:].rearrange("p (r s) -> p s r", r=PACK),
             key_pool[:].bitcast(U32).indirect(k_list[:]),
         )
-        later_codes = sb.tile([P, NQ - CHUNK], U32, name="later_codes", tag="after_moves", align_bytes=64)
+        q_codes = sb.tile([P, NQ], U32, name="q_codes", tag="after_moves", align_bytes=64)
         for a, b in ((CHUNK, HALF), (HALF, NQ)):
-            nc.vector.quantize_mx(
-                later_codes[:, a - CHUNK : b - CHUNK].bitcast(FP8X4), q_scales[:, a:b], woven[:, a * PACK : b * PACK]
-            )
+            nc.vector.quantize_mx(q_codes[:, a:b].bitcast(FP8X4), q_scales[:, a:b], woven[:, a * PACK : b * PACK])
+        nc.vector.tensor_copy(q_codes[:, :CHUNK], first_codes[:])
 
         y_codes = sb.tile([P, NQ], I32, name="y_codes", align_bytes=64)
         y_scales = sb.tile([P, NQ], U8, name="y_scales", align_bytes=64)
@@ -150,7 +149,7 @@ def tile_attend_plw_lq_topk_kernel(tc, qT, k_words, k_scales, ls, offq, offs, ou
         shifted = [sb.tile([P, PACK, HALF], F32, name=f"shifted{h}") for h in range(2)]
 
         def codes(a, b):
-            return later_codes[:, a - CHUNK : b - CHUNK] if a else first_codes[:]
+            return first_codes[:] if b == CHUNK else q_codes[:, a:b]
 
         def scores(r0, r1, a, b, width, tag=None):
             h, o = divmod(a, HALF)
@@ -182,27 +181,30 @@ def tile_attend_plw_lq_topk_kernel(tc, qT, k_words, k_scales, ls, offq, offs, ou
             nc.vector.quantize_mx(y_codes[:, a:b].bitcast(FP8X4), y_scales[:, a:b], tile)
 
         for c in (0, CHUNK):
-            scores(0, 2, c, c + CHUNK, CHUNK)
+            for r in (0, 1):
+                scores(r, r + 1, c, c + CHUNK, CHUNK)
         store(0, 2, 0)
         for r in (0, 1):
             scores(r, r + 1, HALF, NQ, HALF)
         store(0, 2, 1)
-        for c in (HALF, NQ - CHUNK):
-            scores(2, 4, c, c + CHUNK, CHUNK)
+        for r, tag in ((2, None), (3, "ls_bank")):
+            scores(r, r + 1, HALF, NQ, HALF, tag=tag)
         store(2, 4, 1)
-        for c in (0, CHUNK):
-            scores(2, 4, c, c + CHUNK, CHUNK, tag=f"bank0_{c}")
+        for r in (2, 3):
+            scores(r, r + 1, 0, HALF, HALF, tag=f"bank{r - 2}_0")
         store(2, 4, 0)
         rounded = sb.tile([P, NQ * PACK], BF16, name="rounded", tag="after_passes", align_bytes=64)
-        woven_y = [rounded[:, c * CHUNK * PACK : (c + 1) * CHUNK * PACK] for c in range(4)]
-        nc.scalar.activation(woven_order(woven_y[1]), row_order(shifted[0][:, :, CHUNK:]), EXP)
-        for c in (2, 3, 0):
-            h, o = divmod(c * CHUNK, HALF)
-            nc.vector.tensor_copy(woven_order(woven_y[c]), row_order(y[h][:, :, o : o + CHUNK]))
+        nc.scalar.activation(
+            woven_order(rounded[:, CHUNK * PACK : HALF * PACK]),
+            row_order(shifted[0][:, :, CHUNK:]),
+            EXP,
+        )
+        nc.vector.tensor_copy(woven_order(rounded[:, HALF * PACK :]), row_order(y[1][:]))
+        nc.vector.tensor_copy(woven_order(rounded[:, : CHUNK * PACK]), row_order(y[0][:, :, :CHUNK]))
         quantise(HALF, NQ, rounded[:, HALF * PACK :])
         nc.sync.dma_start(words_out[:, HALF:], y_codes[:, HALF:])
-        quantise(0, CHUNK, woven_y[0])
-        quantise(CHUNK, HALF, woven_y[1])
+        for a in (0, CHUNK):
+            quantise(a, a + CHUNK, rounded[:, a * PACK : (a + CHUNK) * PACK])
         nc.sync.dma_start(words_out[:, :HALF], y_codes[:, :HALF])
         scale_rows = out_2[0].rearrange("(g j) q -> j g q", j=4)
         for j in range(4):

@@ -23,9 +23,13 @@ NQ = 512
 N = 512
 HALF = NQ // 2
 CHUNK = 128
+LIST_ROWS = 16
+SCALE_ROWS = D // 32
+QUADRANTS = 4
 SPLIT = 768
 ON_SCALAR = ((288, 96), (352, 72))
-ROW0 = P - 16
+ROW0 = P - SCALE_ROWS
+BANKS = 7
 
 FLOPS = 2 * D * N * NQ
 
@@ -45,11 +49,11 @@ def tile_attend_plw_lq_topk_kernel(tc, qT, k_words, k_scales, ls, offq, offs, ou
 
         scale_pool = sb.tile([P, POOL_K], U8, name="scale_pool")
         nc.gpsimd.memset(scale_pool[:ROW0, :].bitcast(I32), 0)
-        k_list = sb.tile([P, N // 16], U16, name="k_list")
+        k_list = sb.tile([P, N // LIST_ROWS], U16, name="k_list")
         nc.sync.dma_start(k_list[:], offs)
         nc.scalar.dma_start(scale_pool[ROW0:, :].bitcast(I32), k_scales[0].bitcast(I32))
         load_q(0, 0, SPLIT)
-        q_list = sb.tile([P, NQ // 16], U16, name="q_list")
+        q_list = sb.tile([P, NQ // LIST_ROWS], U16, name="q_list")
         nc.sync.dma_start(q_list[:], offq)
         load_q(0, SPLIT, POOL_Q)
         load_q(1, 0, SPLIT)
@@ -72,7 +76,7 @@ def tile_attend_plw_lq_topk_kernel(tc, qT, k_words, k_scales, ls, offq, offs, ou
             ks_rows[:].rearrange("p (r s) -> p r s", r=PACK),
             ks_listed[:].rearrange("p (s r) -> p r s", r=PACK),
         )
-        for g in range(4):
+        for g in range(QUADRANTS):
             nc.sync.dma_start(
                 ks_dealt[32 * g : 32 * g + 4, :].bitcast(I32), ks_rows[ROW0 + 4 * g : ROW0 + 4 * g + 4, :].bitcast(I32)
             )
@@ -84,16 +88,15 @@ def tile_attend_plw_lq_topk_kernel(tc, qT, k_words, k_scales, ls, offq, offs, ou
             nc.scalar.activation(
                 pairs[u][:, a : a + split, :], raw[u, a][:, :, :split].rearrange("p t c -> p c t"), COPY
             )
-            if split < width:
-                nc.vector.tensor_copy(
-                    pairs[u][:, a + split : a + width, :], raw[u, a][:, :, split:].rearrange("p t c -> p c t")
-                )
+            nc.vector.tensor_copy(
+                pairs[u][:, a + split : a + width, :], raw[u, a][:, :, split:].rearrange("p t c -> p c t")
+            )
 
         listed = sb.tile([P, 2, NQ], U32, name="listed")
 
         def gather_q(u, a, b):
             window = pairs[u][:].rearrange("p c t -> p (c t)").bitcast(U32)
-            nc.vector.tensor_copy(listed[:, u, a:b], window.indirect(q_list[:, a // 16 : b // 16]))
+            nc.vector.tensor_copy(listed[:, u, a:b], window.indirect(q_list[:, a // LIST_ROWS : b // LIST_ROWS]))
 
         cast(0, 0, ON_SCALAR[0][0])
         cast(0, SPLIT, ON_SCALAR[0][1])
@@ -130,7 +133,7 @@ def tile_attend_plw_lq_topk_kernel(tc, qT, k_words, k_scales, ls, offq, offs, ou
             key_pool[:].bitcast(U32).indirect(k_list[:]),
         )
         q_codes = sb.tile([P, NQ], U32, name="q_codes", tag="after_moves", align_bytes=64)
-        for a, b in ((CHUNK, HALF), (HALF, NQ)):
+        for a, b in ((CHUNK, HALF), (HALF, HALF + CHUNK), (HALF + CHUNK, NQ)):
             nc.vector.quantize_mx(q_codes[:, a:b].bitcast(FP8X4), q_scales[:, a:b], woven[:, a * PACK : b * PACK])
         nc.vector.tensor_copy(q_codes[:, :CHUNK], first_codes[:])
 
@@ -145,62 +148,44 @@ def tile_attend_plw_lq_topk_kernel(tc, qT, k_words, k_scales, ls, offq, offs, ou
         def row_order(tile):
             return tile.rearrange("p t (a i) -> p a t i", i=4)
 
-        y = [sb.tile([P, PACK, HALF], F32, name=f"y{h}") for h in range(2)]
-        shifted = [sb.tile([P, PACK, HALF], F32, name=f"shifted{h}") for h in range(2)]
+        y = sb.tile([P, PACK, NQ], F32, name="y")
+        shifted = sb.tile([P, PACK, NQ], F32, name="shifted")
 
-        def codes(a, b):
-            return first_codes[:] if b == CHUNK else q_codes[:, a:b]
-
-        def scores(r0, r1, a, b, width, tag=None):
-            h, o = divmod(a, HALF)
-            name = f"bank{r0}_{a}"
-            bank = ps.tile([P, r1 - r0, b - a], F32, name=name, tag=tag or name)
-            for r in range(r0, r1):
-                for c in range(a, b, width):
-                    nc.tensor.matmul_mx(
-                        bank[:, r - r0, c - a : c - a + width],
-                        lhsT=kw_dealt[:, r * P : (r + 1) * P].bitcast(FP8X4),
-                        lhsT_scale=ks_dealt[:, r * P : (r + 1) * P],
-                        rhs=codes(c, c + width).bitcast(FP8X4),
-                        rhs_scale=q_scales[:, c : c + width],
-                        start=True,
-                        stop=True,
-                    )
-            nc.vector.tensor_tensor(
-                shifted[h][:, r0:r1, o : o + b - a],
+        def scores(r, a, b, tag):
+            bank = ps.tile([P, b - a], F32, name=f"bank{r}_{a}", tag=tag)
+            nc.tensor.matmul_mx(
                 bank[:],
-                ls_rows[:, a:b].unsqueeze(1).to_broadcast([P, r1 - r0, b - a]),
-                SUB,
+                lhsT=kw_dealt[:, r * P : (r + 1) * P].bitcast(FP8X4),
+                lhsT_scale=ks_dealt[:, r * P : (r + 1) * P],
+                rhs=(first_codes[:] if b == CHUNK else q_codes[:, a:b]).bitcast(FP8X4),
+                rhs_scale=q_scales[:, a:b],
+                start=True,
+                stop=True,
             )
-            nc.scalar.activation(y[h][:, r0:r1, o : o + b - a], shifted[h][:, r0:r1, o : o + b - a], EXP)
-
-        def store(r0, r1, h):
-            nc.sync.dma_start(y_rows[:, r0:r1, h * HALF : (h + 1) * HALF], y[h][:, r0:r1, :])
+            nc.vector.tensor_tensor(shifted[:, r, a:b], bank[:], ls_rows[:, a:b], SUB)
+            nc.scalar.activation(y[:, r, a:b], shifted[:, r, a:b], EXP)
 
         def quantise(a, b, tile):
             nc.vector.quantize_mx(y_codes[:, a:b].bitcast(FP8X4), y_scales[:, a:b], tile)
 
-        for c in (0, CHUNK):
-            for r in (0, 1):
-                scores(r, r + 1, c, c + CHUNK, CHUNK)
-        store(0, 2, 0)
-        for r in (0, 1):
-            scores(r, r + 1, HALF, NQ, HALF)
-        store(0, 2, 1)
-        for r, tag in ((2, None), (3, "ls_bank")):
-            scores(r, r + 1, HALF, NQ, HALF, tag=tag)
-        store(2, 4, 1)
-        for r in (2, 3):
-            scores(r, r + 1, 0, HALF, HALF, tag=f"bank{r - 2}_0")
-        store(2, 4, 0)
+        first, second = (0, HALF), (HALF, NQ)
+        passes = [(0, a, a + CHUNK) for a in range(0, NQ, CHUNK)] + [(1, *second), (1, *first)]
+        passes = passes + [(r, *span) for span in (second, first) for r in (2, 3)]
+        done = [0] * PACK
+        for count, (r, a, b) in enumerate(passes):
+            scores(r, a, b, f"turn{count % BANKS}")
+            done[r] = done[r] + b - a
+            if done[r] == NQ:
+                nc.sync.dma_start(y_rows[:, r, :], y[:, r, :])
+
         rounded = sb.tile([P, NQ * PACK], BF16, name="rounded", tag="after_passes", align_bytes=64)
         nc.scalar.activation(
             woven_order(rounded[:, CHUNK * PACK : HALF * PACK]),
-            row_order(shifted[0][:, :, CHUNK:]),
+            row_order(shifted[:, :, CHUNK:HALF]),
             EXP,
         )
-        nc.vector.tensor_copy(woven_order(rounded[:, HALF * PACK :]), row_order(y[1][:]))
-        nc.vector.tensor_copy(woven_order(rounded[:, : CHUNK * PACK]), row_order(y[0][:, :, :CHUNK]))
+        nc.vector.tensor_copy(woven_order(rounded[:, HALF * PACK :]), row_order(y[:, :, HALF:NQ]))
+        nc.vector.tensor_copy(woven_order(rounded[:, : CHUNK * PACK]), row_order(y[:, :, 0:CHUNK]))
         quantise(HALF, NQ, rounded[:, HALF * PACK :])
         nc.sync.dma_start(words_out[:, HALF:], y_codes[:, HALF:])
         for a in (0, CHUNK):

@@ -28,6 +28,7 @@ SCALE_ROWS = D // 32
 QUADRANTS = 4
 SPLIT = 768
 ON_SCALAR = ((288, 96), (352, 72))
+ON_VECTOR = 104
 ROW0 = P - SCALE_ROWS
 BANKS = 7
 
@@ -169,27 +170,27 @@ def tile_attend_plw_lq_topk_kernel(tc, qT, k_words, k_scales, ls, offq, offs, ou
             nc.vector.quantize_mx(y_codes[:, a:b].bitcast(FP8X4), y_scales[:, a:b], tile)
 
         first, second = (0, HALF), (HALF, NQ)
-        passes = [(0, a, a + CHUNK) for a in range(0, NQ, CHUNK)] + [(1, *second), (1, *first)]
-        passes = passes + [(r, *span) for span in (second, first) for r in (2, 3)]
-        done = [0] * PACK
-        for count, (r, a, b) in enumerate(passes):
-            scores(r, a, b, f"turn{count % BANKS}")
-            done[r] = done[r] + b - a
-            if done[r] == NQ:
-                nc.sync.dma_start(y_rows[:, r, :], y[:, r, :])
+        groups = [([(0, a, a + CHUNK) for a in range(0, NQ, CHUNK)], (0, 1, 0, NQ))]
+        groups = groups + [([(1, *span)], (1, 2, *span)) for span in (second, first)]
+        groups = groups + [([(2, *span), (3, *span)], (2, PACK, *span)) for span in (second, first)]
+        count = 0
+        for passes, (r0, r1, q0, q1) in groups:
+            for r, a, b in passes:
+                scores(r, a, b, f"turn{count % BANKS}")
+                count = count + 1
+            nc.sync.dma_start(y_rows[:, r0:r1, q0:q1], y[:, r0:r1, q0:q1])
 
         rounded = sb.tile([P, NQ * PACK], BF16, name="rounded", tag="after_passes", align_bytes=64)
         nc.scalar.activation(
-            woven_order(rounded[:, CHUNK * PACK : HALF * PACK]),
-            row_order(shifted[:, :, CHUNK:HALF]),
+            woven_order(rounded[:, ON_VECTOR * PACK : HALF * PACK]),
+            row_order(shifted[:, :, ON_VECTOR:HALF]),
             EXP,
         )
         nc.vector.tensor_copy(woven_order(rounded[:, HALF * PACK :]), row_order(y[:, :, HALF:NQ]))
-        nc.vector.tensor_copy(woven_order(rounded[:, : CHUNK * PACK]), row_order(y[:, :, 0:CHUNK]))
+        nc.vector.tensor_copy(woven_order(rounded[:, : ON_VECTOR * PACK]), row_order(y[:, :, 0:ON_VECTOR]))
         quantise(HALF, NQ, rounded[:, HALF * PACK :])
         nc.sync.dma_start(words_out[:, HALF:], y_codes[:, HALF:])
-        for a in (0, CHUNK):
-            quantise(a, a + CHUNK, rounded[:, a * PACK : (a + CHUNK) * PACK])
+        quantise(0, HALF, rounded[:, : HALF * PACK])
         nc.sync.dma_start(words_out[:, :HALF], y_codes[:, :HALF])
         scale_rows = out_2[0].rearrange("(g j) q -> j g q", j=4)
         for j in range(4):

@@ -45,7 +45,7 @@ def tile_attend_plw_lq_topk_kernel(tc, qT, k_words, k_scales, ls, offq, offs, ou
         raw = {}
 
         def load_q(u, a, b):
-            raw[u, a] = sb.tile([P, 2, b - a], F32, name=f"raw{u}_{a}")
+            raw[u, a] = sb.tile([P, 2, b - a], F32, name=f"raw{u}_{a}", tag=f"raw{u}_{a}")
             nc.sync.dma_start(raw[u, a][:], q_rows[:, 2 * u : 2 * u + 2, a:b])
 
         scale_pool = sb.tile([P, POOL_K], U8, name="scale_pool")
@@ -56,14 +56,14 @@ def tile_attend_plw_lq_topk_kernel(tc, qT, k_words, k_scales, ls, offq, offs, ou
         load_q(0, 0, SPLIT)
         q_list = sb.tile([P, NQ // LIST_ROWS], U16, name="q_list")
         nc.sync.dma_start(q_list[:], offq)
+        ls_four = sb.tile([P, P], F32, name="ls_four")
+        nc.vector.memset(ls_four[: P - PACK, :], 0.0)
+        nc.sync.dma_start(ls_four[P - PACK :, :], ls.rearrange("a b (c n) -> (a b c) n", c=PACK))
         load_q(0, SPLIT, POOL_Q)
         load_q(1, 0, SPLIT)
         load_q(1, SPLIT, POOL_Q)
         key_pool = sb.tile([P, POOL_K], I32, name="key_pool")
         nc.sync.dma_start(key_pool[:], k_words[0].rearrange("p n t -> p (n t)").bitcast(I32))
-
-        ls_cols = sb.tile([P, PACK], F32, name="ls_cols")
-        nc.sync.dma_start(ls_cols[:], ls.rearrange("a b (p c) -> p (a b c)", c=PACK))
 
         ident = sb.tile([P, P], F32, name="ident")
         make_identity(nc, ident[:])
@@ -93,7 +93,7 @@ def tile_attend_plw_lq_topk_kernel(tc, qT, k_words, k_scales, ls, offq, offs, ou
                 pairs[u][:, a + split : a + width, :], raw[u, a][:, :, split:].rearrange("p t c -> p c t")
             )
 
-        listed = sb.tile([P, 2, NQ], U32, name="listed")
+        listed = sb.tile([P, 2, NQ], U32, name="listed", tag="after_weave")
 
         def gather_q(u, a, b):
             window = pairs[u][:].rearrange("p c t -> p (c t)").bitcast(U32)
@@ -102,6 +102,14 @@ def tile_attend_plw_lq_topk_kernel(tc, qT, k_words, k_scales, ls, offq, offs, ou
         cast(0, 0, ON_SCALAR[0][0])
         cast(0, SPLIT, ON_SCALAR[0][1])
         gather_q(0, 0, NQ)
+
+        ls_turned = ps.tile([P, P], F32, name="ls_turned", tag=f"turn{BANKS - 1}")
+        nc.tensor.transpose(ls_turned[:], ls_four[:], ident[:])
+        ls_cols = sb.tile([P, PACK], F32, name="ls_cols", tag=f"raw0_{SPLIT}")
+        nc.scalar.copy(ls_cols[:], ls_turned[:, P - PACK :])
+        ls_bank = ps.tile([P, PACK, P], F32, name="ls_bank")
+        for c in range(PACK):
+            nc.tensor.transpose(ls_bank[:, c, :], ls_cols[:, c : c + 1].to_broadcast([P, P]), ident[:])
 
         cast(1, 0, ON_SCALAR[1][0])
         cast(1, SPLIT, ON_SCALAR[1][1])
@@ -115,15 +123,8 @@ def tile_attend_plw_lq_topk_kernel(tc, qT, k_words, k_scales, ls, offq, offs, ou
                 listed[:, :, a:b].rearrange("p u c -> p c u"),
             )
 
-        ls_bank = ps.tile([P, PACK, P], F32, name="ls_bank")
-        for c in range(PACK):
-            nc.tensor.transpose(ls_bank[:, c, :], ls_cols[:, c : c + 1].to_broadcast([P, P]), ident[:])
-        ls_rows = sb.tile([P, NQ], F32, name="ls_rows")
-        for a, b in ((0, CHUNK), (CHUNK, NQ)):
-            nc.scalar.copy(
-                ls_rows[:, a:b].rearrange("p (n c) -> p n c", c=PACK),
-                ls_bank[:, :, a // PACK : b // PACK].rearrange("p c n -> p n c"),
-            )
+        ls_rows = sb.tile([P, NQ], F32, name="ls_rows", tag="after_weave")
+        nc.scalar.copy(ls_rows[:], ls_bank[:].rearrange("p c n -> p (c n)"))
 
         q_scales = sb.tile([P, NQ], U8, name="q_scales", align_bytes=64)
         first_codes = sb.tile([P, CHUNK], U32, name="first_codes", align_bytes=64)
@@ -194,5 +195,5 @@ def tile_attend_plw_lq_topk_kernel(tc, qT, k_words, k_scales, ls, offq, offs, ou
         nc.sync.dma_start(words_out[:, :HALF], y_codes[:, :HALF])
         scale_rows = out_2[0].rearrange("(g j) q -> j g q", j=4)
         for j in range(4):
-            queue = nc.sync if j % 2 else nc.scalar
+            queue = nc.scalar if j % 2 else nc.sync
             queue.dma_start(scale_rows[j].bitcast(I32), y_scales[j:P:32, :].bitcast(I32))

@@ -28,7 +28,6 @@ SCALE_ROWS = D // 32
 QUADRANTS = 4
 SPLIT = 768
 ON_SCALAR = ((288, 96), (352, 72))
-ON_VECTOR = 104
 ROW0 = P - SCALE_ROWS
 BANKS = 7
 
@@ -172,7 +171,7 @@ def tile_attend_plw_lq_topk_kernel(tc, qT, k_words, k_scales, ls, offq, offs, ou
 
         first, second = (0, HALF), (HALF, NQ)
         groups = [([(0, a, a + CHUNK) for a in range(0, NQ, CHUNK)], (0, 1, 0, NQ))]
-        groups = groups + [([(1, *span)], (1, 2, *span)) for span in (second, first)]
+        groups = groups + [([(1, *second), (1, *first)], (1, 2, 0, NQ))]
         groups = groups + [([(2, *span), (3, *span)], (2, PACK, *span)) for span in (second, first)]
         count = 0
         for passes, (r0, r1, q0, q1) in groups:
@@ -182,17 +181,12 @@ def tile_attend_plw_lq_topk_kernel(tc, qT, k_words, k_scales, ls, offq, offs, ou
             nc.sync.dma_start(y_rows[:, r0:r1, q0:q1], y[:, r0:r1, q0:q1])
 
         rounded = sb.tile([P, NQ * PACK], BF16, name="rounded", tag="after_passes", align_bytes=64)
-        nc.scalar.activation(
-            woven_order(rounded[:, ON_VECTOR * PACK : HALF * PACK]),
-            row_order(shifted[:, :, ON_VECTOR:HALF]),
-            EXP,
-        )
-        nc.vector.tensor_copy(woven_order(rounded[:, HALF * PACK :]), row_order(y[:, :, HALF:NQ]))
-        nc.vector.tensor_copy(woven_order(rounded[:, : ON_VECTOR * PACK]), row_order(y[:, :, 0:ON_VECTOR]))
-        quantise(HALF, NQ, rounded[:, HALF * PACK :])
-        nc.sync.dma_start(words_out[:, HALF:], y_codes[:, HALF:])
-        quantise(0, HALF, rounded[:, : HALF * PACK])
-        nc.sync.dma_start(words_out[:, :HALF], y_codes[:, :HALF])
+        nc.scalar.activation(woven_order(rounded[:, : CHUNK * PACK]), row_order(shifted[:, :, :CHUNK]), EXP)
+        for a, b in (second, (CHUNK, HALF)):
+            nc.vector.tensor_copy(woven_order(rounded[:, a * PACK : b * PACK]), row_order(y[:, :, a:b]))
+        for a, b in (second, (CHUNK, HALF), (0, CHUNK)):
+            quantise(a, b, rounded[:, a * PACK : b * PACK])
+            nc.sync.dma_start(words_out[:, a:b], y_codes[:, a:b])
         scale_rows = out_2[0].rearrange("(g j) q -> j g q", j=4)
         for j in range(4):
             queue = nc.scalar if j % 2 else nc.sync

@@ -158,7 +158,7 @@ def tile_attend_plw_lq_topk_kernel(tc, qT, k_words, k_scales, ls, offq, offs, ou
                 bank[:],
                 lhsT=kw_dealt[:, r * P : (r + 1) * P].bitcast(FP8X4),
                 lhsT_scale=ks_dealt[:, r * P : (r + 1) * P],
-                rhs=(first_codes[:] if b == CHUNK else q_codes[:, a:b]).bitcast(FP8X4),
+                rhs=(first_codes[:] if (r, b) == (0, CHUNK) else q_codes[:, a:b]).bitcast(FP8X4),
                 rhs_scale=q_scales[:, a:b],
                 start=True,
                 stop=True,
@@ -170,9 +170,10 @@ def tile_attend_plw_lq_topk_kernel(tc, qT, k_words, k_scales, ls, offq, offs, ou
             nc.vector.quantize_mx(y_codes[:, a:b].bitcast(FP8X4), y_scales[:, a:b], tile)
 
         first, second = (0, HALF), (HALF, NQ)
-        groups = [([(0, a, a + CHUNK) for a in range(0, NQ, CHUNK)], (0, 1, 0, NQ))]
+        groups = [([(0, a, a + CHUNK), (0, a + CHUNK, b)], (0, 1, a, b)) for a, b in (first, second)]
         groups = groups + [([(1, *second), (1, *first)], (1, 2, 0, NQ))]
-        groups = groups + [([(2, *span), (3, *span)], (2, PACK, *span)) for span in (second, first)]
+        groups = groups + [([(2, *second), (3, *second)], (2, PACK, *second))]
+        groups = groups + [([(2, *first), (3, CHUNK, HALF), (3, 0, CHUNK)], (2, PACK, *first))]
         count = 0
         for passes, (r0, r1, q0, q1) in groups:
             for r, a, b in passes:
@@ -184,10 +185,12 @@ def tile_attend_plw_lq_topk_kernel(tc, qT, k_words, k_scales, ls, offq, offs, ou
         nc.scalar.activation(woven_order(rounded[:, : CHUNK * PACK]), row_order(shifted[:, :, :CHUNK]), EXP)
         for a, b in (second, (CHUNK, HALF)):
             nc.vector.tensor_copy(woven_order(rounded[:, a * PACK : b * PACK]), row_order(y[:, :, a:b]))
-        for a, b in (second, (CHUNK, HALF), (0, CHUNK)):
+        quantise(*second, rounded[:, HALF * PACK :])
+        nc.scalar.dma_start(words_out[:, HALF:], y_codes[:, HALF:])
+        for a, b in ((CHUNK, HALF), (0, CHUNK)):
             quantise(a, b, rounded[:, a * PACK : b * PACK])
-            nc.sync.dma_start(words_out[:, a:b], y_codes[:, a:b])
+        nc.scalar.dma_start(words_out[:, :HALF], y_codes[:, :HALF])
         scale_rows = out_2[0].rearrange("(g j) q -> j g q", j=4)
         for j in range(4):
-            queue = nc.scalar if j % 2 else nc.sync
+            queue = nc.scalar if j == 3 else nc.sync
             queue.dma_start(scale_rows[j].bitcast(I32), y_scales[j:P:32, :].bitcast(I32))

from contextlib import ExitStack

import concourse.mybir as mybir
from concourse.masks import make_identity

F32 = mybir.dt.float32
BF16 = mybir.dt.bfloat16
I32 = mybir.dt.int32
U32 = mybir.dt.uint32
U16 = mybir.dt.uint16
U8 = mybir.dt.uint8
FP8X4 = mybir.dt.float8_e4m3fn_x4
COPY = mybir.ActivationFunctionType.Copy
EXP = mybir.ActivationFunctionType.Exp
SUB = mybir.AluOpType.subtract

P = 128
PACK = 4
D = 512
POOL_Q = 1024
POOL_K = 2048
NQ = 512
N = 512
HALF = NQ // 2
CHUNK = 128
LIST_ROWS = 16
SCALE_ROWS = D // 32
QUADRANTS = 4
SPLIT = 768
ON_SCALAR = ((288, 96), (352, 72))
ROW0 = P - SCALE_ROWS
BANKS = 7

FLOPS = 2 * D * N * NQ


def tile_attend_plw_lq_topk_kernel(tc, qT, k_words, k_scales, ls, offq, offs, out_0, out_1, out_2):
    nc = tc.nc
    with ExitStack() as ctx:
        sb = ctx.enter_context(tc.tile_pool(name="sb", bufs=1))
        ps = ctx.enter_context(tc.psum_pool(name="ps", bufs=1))

        q_rows = qT.rearrange("(p t) c -> p t c", t=PACK)
        raw = {}

        def load_q(u, a, b):
            raw[u, a] = sb.tile([P, 2, b - a], F32, name=f"raw{u}_{a}", tag=f"raw{u}_{a}")
            nc.sync.dma_start(raw[u, a][:], q_rows[:, 2 * u : 2 * u + 2, a:b])

        scale_pool = sb.tile([P, POOL_K], U8, name="scale_pool")
        nc.gpsimd.memset(scale_pool[:ROW0, :].bitcast(I32), 0)
        k_list = sb.tile([P, N // LIST_ROWS], U16, name="k_list")
        nc.sync.dma_start(k_list[:], offs)
        nc.scalar.dma_start(scale_pool[ROW0:, :].bitcast(I32), k_scales[0].bitcast(I32))
        load_q(0, 0, SPLIT)
        q_list = sb.tile([P, NQ // LIST_ROWS], U16, name="q_list")
        nc.sync.dma_start(q_list[:], offq)
        ls_four = sb.tile([P, P], F32, name="ls_four")
        nc.vector.memset(ls_four[: P - PACK, :], 0.0)
        nc.sync.dma_start(ls_four[P - PACK :, :], ls.rearrange("a b (c n) -> (a b c) n", c=PACK))
        load_q(0, SPLIT, POOL_Q)
        load_q(1, 0, SPLIT)
        load_q(1, SPLIT, POOL_Q)
        key_pool = sb.tile([P, POOL_K], I32, name="key_pool")
        nc.sync.dma_start(key_pool[:], k_words[0].rearrange("p n t -> p (n t)").bitcast(I32))

        ident = sb.tile([P, P], F32, name="ident")
        make_identity(nc, ident[:])

        ks_listed = sb.tile([P, N], U8, name="ks_listed")
        nc.vector.tensor_copy(ks_listed[:], scale_pool[:].indirect(k_list[:]))
        ks_dealt = sb.tile([P, N], U8, name="ks_dealt", align_bytes=64)
        nc.gpsimd.memset(ks_dealt[:].bitcast(I32), 0)
        ks_rows = sb.tile([P, N], U8, name="ks_rows", tag="after_moves", align_bytes=64)
        nc.vector.tensor_copy(
            ks_rows[:].rearrange("p (r s) -> p r s", r=PACK),
            ks_listed[:].rearrange("p (s r) -> p r s", r=PACK),
        )
        for g in range(QUADRANTS):
            nc.sync.dma_start(
                ks_dealt[32 * g : 32 * g + 4, :].bitcast(I32), ks_rows[ROW0 + 4 * g : ROW0 + 4 * g + 4, :].bitcast(I32)
            )

        pairs = [sb.tile([P, POOL_Q, 2], BF16, name=f"pairs{u}") for u in range(2)]

        def cast(u, a, split):
            width = raw[u, a].shape[2]
            nc.scalar.activation(
                pairs[u][:, a : a + split, :], raw[u, a][:, :, :split].rearrange("p t c -> p c t"), COPY
            )
            nc.vector.tensor_copy(
                pairs[u][:, a + split : a + width, :], raw[u, a][:, :, split:].rearrange("p t c -> p c t")
            )

        listed = sb.tile([P, 2, NQ], U32, name="listed", tag="after_weave")

        def gather_q(u, a, b):
            window = pairs[u][:].rearrange("p c t -> p (c t)").bitcast(U32)
            nc.vector.tensor_copy(listed[:, u, a:b], window.indirect(q_list[:, a // LIST_ROWS : b // LIST_ROWS]))

        cast(0, 0, ON_SCALAR[0][0])
        cast(0, SPLIT, ON_SCALAR[0][1])
        gather_q(0, 0, NQ)

        ls_turned = ps.tile([P, P], F32, name="ls_turned", tag=f"turn{BANKS - 1}")
        nc.tensor.transpose(ls_turned[:], ls_four[:], ident[:])
        ls_cols = sb.tile([P, PACK], F32, name="ls_cols", tag=f"raw0_{SPLIT}")
        nc.scalar.copy(ls_cols[:], ls_turned[:, P - PACK :])
        ls_bank = ps.tile([P, PACK, P], F32, name="ls_bank")
        for c in range(PACK):
            nc.tensor.transpose(ls_bank[:, c, :], ls_cols[:, c : c + 1].to_broadcast([P, P]), ident[:])

        cast(1, 0, ON_SCALAR[1][0])
        cast(1, SPLIT, ON_SCALAR[1][1])
        gather_q(1, 0, CHUNK)
        gather_q(1, CHUNK, NQ)

        woven = sb.tile([P, NQ * PACK], BF16, name="woven", align_bytes=64)
        for a, b in ((0, CHUNK), (CHUNK, HALF), (HALF, NQ)):
            nc.scalar.copy(
                woven[:, a * PACK : b * PACK].bitcast(U32).rearrange("p (c u) -> p c u", u=2),
                listed[:, :, a:b].rearrange("p u c -> p c u"),
            )

        ls_rows = sb.tile([P, NQ], F32, name="ls_rows", tag="after_weave")
        nc.scalar.copy(ls_rows[:], ls_bank[:].rearrange("p c n -> p (c n)"))

        q_scales = sb.tile([P, NQ], U8, name="q_scales", align_bytes=64)
        first_codes = sb.tile([P, CHUNK], U32, name="first_codes", align_bytes=64)
        nc.vector.quantize_mx(first_codes[:].bitcast(FP8X4), q_scales[:, :CHUNK], woven[:, : CHUNK * PACK])
        kw_dealt = sb.tile([P, N], U32, name="kw_dealt", tag="after_passes", align_bytes=64)
        nc.vector.tensor_copy(
            kw_dealt[:].rearrange("p (r s) -> p s r", r=PACK),
            key_pool[:].bitcast(U32).indirect(k_list[:]),
        )
        q_codes = sb.tile([P, NQ], U32, name="q_codes", tag="after_moves", align_bytes=64)
        for a, b in ((CHUNK, HALF), (HALF, HALF + CHUNK), (HALF + CHUNK, NQ)):
            nc.vector.quantize_mx(q_codes[:, a:b].bitcast(FP8X4), q_scales[:, a:b], woven[:, a * PACK : b * PACK])
        nc.vector.tensor_copy(q_codes[:, :CHUNK], first_codes[:])

        y_codes = sb.tile([P, NQ], I32, name="y_codes", align_bytes=64)
        y_scales = sb.tile([P, NQ], U8, name="y_scales", align_bytes=64)
        y_rows = out_0.rearrange("(s r) q -> s r q", r=PACK)
        words_out = out_1[0].rearrange("p q t -> p (q t)").bitcast(I32)

        def woven_order(tile):
            return tile.rearrange("p (a i t) -> p a t i", i=4, t=PACK)

        def row_order(tile):
            return tile.rearrange("p t (a i) -> p a t i", i=4)

        y = sb.tile([P, PACK, NQ], F32, name="y")
        shifted = sb.tile([P, PACK, NQ], F32, name="shifted")

        def scores(r, a, b, tag):
            bank = ps.tile([P, b - a], F32, name=f"bank{r}_{a}", tag=tag)
            nc.tensor.matmul_mx(
                bank[:],
                lhsT=kw_dealt[:, r * P : (r + 1) * P].bitcast(FP8X4),
                lhsT_scale=ks_dealt[:, r * P : (r + 1) * P],
                rhs=(first_codes[:] if (r, b) == (0, CHUNK) else q_codes[:, a:b]).bitcast(FP8X4),
                rhs_scale=q_scales[:, a:b],
                start=True,
                stop=True,
            )
            nc.vector.tensor_tensor(shifted[:, r, a:b], bank[:], ls_rows[:, a:b], SUB)
            nc.scalar.activation(y[:, r, a:b], shifted[:, r, a:b], EXP)

        def quantise(a, b, tile):
            nc.vector.quantize_mx(y_codes[:, a:b].bitcast(FP8X4), y_scales[:, a:b], tile)

        first, second = (0, HALF), (HALF, NQ)
        groups = [([(0, a, a + CHUNK), (0, a + CHUNK, b)], (0, 1, a, b)) for a, b in (first, second)]
        groups = groups + [([(1, *second), (1, *first)], (1, 2, 0, NQ))]
        groups = groups + [([(2, *second), (3, *second)], (2, PACK, *second))]
        groups = groups + [([(2, *first), (3, CHUNK, HALF), (3, 0, CHUNK)], (2, PACK, *first))]
        count = 0
        for passes, (r0, r1, q0, q1) in groups:
            for r, a, b in passes:
                scores(r, a, b, f"turn{count % BANKS}")
                count = count + 1
            nc.sync.dma_start(y_rows[:, r0:r1, q0:q1], y[:, r0:r1, q0:q1])

        rounded = sb.tile([P, NQ * PACK], BF16, name="rounded", tag="after_passes", align_bytes=64)
        nc.scalar.activation(woven_order(rounded[:, : CHUNK * PACK]), row_order(shifted[:, :, :CHUNK]), EXP)
        for a, b in (second, (CHUNK, HALF)):
            nc.vector.tensor_copy(woven_order(rounded[:, a * PACK : b * PACK]), row_order(y[:, :, a:b]))
        quantise(*second, rounded[:, HALF * PACK :])
        nc.scalar.dma_start(words_out[:, HALF:], y_codes[:, HALF:])
        for a, b in ((CHUNK, HALF), (0, CHUNK)):
            quantise(a, b, rounded[:, a * PACK : b * PACK])
        nc.scalar.dma_start(words_out[:, :HALF], y_codes[:, :HALF])
        scale_rows = out_2[0].rearrange("(g j) q -> j g q", j=4)
        for j in range(4):
            queue = nc.scalar if j == 3 else nc.sync
            queue.dma_start(scale_rows[j].bitcast(I32), y_scales[j:P:32, :].bitcast(I32))
